import numpy as np
import ml_dtypes


def mxq(x, axis, fmt="e4m3"):
    dtype, down = {"e4m3": (ml_dtypes.float8_e4m3fn, 7), "e5m2": (ml_dtypes.float8_e5m2, 14)}[fmt]
    v = np.moveaxis(np.asarray(x, np.float32).astype(ml_dtypes.bfloat16).astype(np.float64), axis, -1)
    blocks = v.reshape(v.shape[:-1] + (-1, 32))
    amax = np.abs(blocks).max(-1, keepdims=True)
    byte = np.maximum(np.where(amax > 0, np.frexp(amax)[1] - 1 + 127, 0) - down, 1)
    scale = np.exp2(byte - 127.0)
    codes = (blocks / scale).astype(np.float32).astype(dtype).astype(np.float64)
    return np.moveaxis((codes * scale).reshape(v.shape), -1, axis)


WIDE = False


def mx_kscale(k):
    if not WIDE:
        return np.ones(k)
    levels = np.array([10, -10, 5, -5, 0])
    if k % 512:
        return np.exp2(np.random.permutation(np.resize(levels, k // 32))).repeat(32)
    a = np.empty((k // 512, 16))
    for p in range(k // 512):
        a[p, :8] = np.random.permutation(np.resize(levels, 8))
        for g in range(8):
            far = levels[np.abs(levels - a[p, g]) >= 10]
            a[p, g + 8] = far[np.random.randint(len(far))]
    return np.exp2(a.ravel()).repeat(32)


def f64(x):
    return np.asarray(x).astype(np.float64)


def striped(idx):
    return np.tile(idx.reshape(-1, 16).T, (8, 1)).astype(np.uint16)


def unstriped(offs):
    return offs[:16].T.reshape(-1).astype(np.int64)


def striped8(idx):
    return np.concatenate([x.reshape(-1, 16).T for x in idx]).astype(np.uint16)


def runs(offs, k):
    lists = np.stack([offs[16 * r : 16 * r + 16].T.reshape(-1) for r in range(8)]).astype(np.int64)
    return lists[np.arange(k) % 512 // 64]


def pack_weight(w):
    k, n = w.shape
    w = f64(np.asarray(w, np.float32).astype(ml_dtypes.bfloat16)).reshape(k // 32, 32, n)
    amax = np.abs(w).max(1)
    byte = np.clip(np.where(amax > 0, np.frexp(amax)[1] - 1 + 127 - 7, 1), 1, 254)
    scaled = (w * np.exp2(127.0 - byte)[:, None, :]).reshape(k, n).astype(np.float32)
    words = np.ascontiguousarray(scaled.reshape(k // 512, 128, 4, n).transpose(0, 1, 3, 2)).astype(ml_dtypes.float8_e4m3fn).view(np.uint8)
    return words, np.ascontiguousarray(byte.astype(np.uint8).reshape(k // 512, 16, n))


def unpack_weight(words, scales):
    g, p, n, _ = words.shape
    vals = np.ascontiguousarray(words).view(ml_dtypes.float8_e4m3fn).astype(np.float64) * np.repeat(np.exp2(scales.astype(np.float64) - 127.0), 8, axis=1)[..., None]
    return vals.transpose(0, 1, 3, 2).reshape(g * 512, n)


E2M1 = np.array([0.0, 0.5, 1.0, 1.5, 2.0, 3.0, 4.0, 6.0, -0.0, -0.5, -1.0, -1.5, -2.0, -3.0, -4.0, -6.0])


def pack_fp4(w):
    k, n = w.shape
    w = f64(np.asarray(w, np.float32).astype(ml_dtypes.bfloat16)).reshape(k // 32, 32, n)
    amax = np.abs(w).max(1)
    mant, ex = np.frexp(amax / 6.0)
    byte = np.clip(np.where(amax > 0, np.where(mant > 0.5, ex, ex - 1) + 127, 1), 1, 254)
    scaled = (w * np.exp2(127.0 - byte)[:, None, :]).reshape(k, n).astype(np.float32)
    c = np.ascontiguousarray(scaled.reshape(k // 512, 128, 4, n).transpose(0, 1, 3, 2)).astype(ml_dtypes.float4_e2m1fn).view(np.uint8) & 0xF
    words = (c[..., 0::2] | (c[..., 1::2] << 4)).reshape(k // 512, 128, 2 * n)
    return np.ascontiguousarray(words), np.ascontiguousarray(byte.astype(np.uint8).reshape(k // 512, 16, n))


def unpack_fp4(words, scales):
    g, _, n = scales.shape
    words = np.ascontiguousarray(words).reshape(g, 128, n, 2)
    nib = np.empty((g, 128, n, 4), np.uint8)
    nib[..., 0::2] = words & 0xF
    nib[..., 1::2] = words >> 4
    vals = E2M1[nib] * np.repeat(np.exp2(scales.astype(np.float64) - 127.0), 8, axis=1)[..., None]
    return vals.transpose(0, 1, 3, 2).reshape(g * 512, n)


def sigmoid(v):
    return 1.0 / (1.0 + np.exp(-np.maximum(v, -700.0)))

def planes(y):
    n, m = y.shape
    v = y.astype(np.float32).astype(ml_dtypes.bfloat16).astype(np.float64).reshape(n // 32, 32, m)
    top = np.abs(v).max(1)
    byte = np.clip(np.where(top > 0, np.frexp(top)[1] - 1 + 127 - 7, 1), 1, 254)
    codes = (v * np.exp2(127.0 - byte)[:, None, :]).reshape(n, m).astype(np.float32).astype(ml_dtypes.float8_e4m3fn).view(np.uint8)
    words = codes.reshape(n // 512, 128, 4, m).transpose(0, 1, 3, 2)
    return np.ascontiguousarray(words), np.ascontiguousarray(byte.astype(np.uint8).reshape(n // 512, 16, m))


K, T, S, V, H, W = 512, 2048, 512, 512, 512, 256


def setup_inputs():
    n = np.random.standard_normal
    s = mx_kscale(K)[:, None]
    u = mx_kscale(S)
    packed_xT = pack_weight(n((K, T)) * s)
    packed_w1 = pack_fp4(n((K, H)) / np.sqrt(K) / s)
    packed_w2 = pack_fp4(n((K, H)) / np.sqrt(K) / s)
    perm = np.stack([np.random.permutation(S) for _ in range(8)])
    return {
        "x_words": packed_xT[0],
        "x_scales": packed_xT[1],
        "w1_words": packed_w1[0],
        "w1_scales": packed_w1[1],
        "w2_words": packed_w2[0],
        "w2_scales": packed_w2[1],
        "ga": (np.random.uniform(0.5, 1.5, (H, 1)) * u[:, None]).astype(np.float32),
        "gb": (np.random.uniform(0.5, 1.5, (H, 1)) / u[:, None]).astype(np.float32),
        "offs": striped(np.random.permutation(T)[:S]),
        "two": striped(np.random.permutation(T)[:V]),
        "n1": striped8(perm[:, :W]),
        "n2": striped8(perm[:, W:]),
        "n3": striped8(np.stack([np.random.permutation(V) for _ in range(8)])),
        "n4": striped8(np.stack([np.random.permutation(V) for _ in range(8)])),
        "n5": striped8(np.stack([np.random.permutation(V) for _ in range(8)])),
        "n6": striped8(np.stack([np.random.permutation(V) for _ in range(8)])),
        "n7": striped8(np.stack([np.random.permutation(V) for _ in range(8)])),
    }


def reference(x_words, x_scales, w1_words, w1_scales, w2_words, w2_scales, ga, gb, offs, two, n1, n2, n3, n4, n5, n6, n7):
    xq = unpack_weight(x_words, x_scales)[:, unstriped(offs)]
    a = unpack_fp4(w1_words, w1_scales).T @ xq
    pa = a[np.arange(H)[:, None], runs(n1, H)]
    pb = a[np.arange(H)[:, None], runs(n2, H)]
    rb = np.minimum(pa, pb)
    ra = np.maximum(pa, pb)
    ds = np.zeros((H, S))
    ds[np.arange(H)[:, None], runs(n1, H)] = ra
    dt = ds.copy()
    dt[np.arange(H)[:, None], runs(n2, H)] = rb
    z = f64(ga) * dt
    x_two = unpack_weight(x_words, x_scales)[:, unstriped(two)]
    b = unpack_fp4(w2_words, w2_scales).T @ x_two
    z2 = f64(gb) * (b * (b[np.arange(H)[:, None], runs(n3, H)] - (b[np.arange(H)[:, None], runs(n4, H)])))
    s = 0.0625 * ((mxq(z, 0, "e4m3").T @ mxq(z2, 0, "e4m3")))
    out_0 = (s[np.arange(S)[:, None], runs(n5, S)]) * sigmoid(s) + (s[np.arange(S)[:, None], runs(n6, S)]) * (sigmoid(s[np.arange(S)[:, None], runs(n7, S)]))
    return (out_0,) + planes(out_0)

@@ -1,0 +1,294 @@
+from contextlib import ExitStack
+
+import concourse.mybir as mybir
+from concourse.masks import make_identity
+
+K, T, S, V, H, W = 512, 2048, 512, 512, 512, 256
+FLOPS = 3 * 2 * 512 * 512 * 512
+
+F32 = mybir.dt.float32
+BF16 = mybir.dt.bfloat16
+I32 = mybir.dt.int32
+U32 = mybir.dt.uint32
+U16 = mybir.dt.uint16
+U8 = mybir.dt.uint8
+FP8X4 = mybir.dt.float8_e4m3fn_x4
+FP4X4 = mybir.dt.float4_e2m1fn_x4
+ALU = mybir.AluOpType
+ACT = mybir.ActivationFunctionType
+
+P = 128
+PACK = 4
+HALF = 256
+QUARTER = 128
+BLOCKS = 16
+CHUNKS = ((0, 256), (256, 384), (384, 512))
+
+
+def tile_picked_kqorderwindwsum_none_po_kernel(tc, x_words, x_scales, w1_words, w1_scales, w2_words, w2_scales, ga, gb, offs, two, n1, n2, n3, n4, n5, n6, n7, out_0, out_1, out_2):
+    nc = tc.nc
+    with ExitStack() as ctx:
+        keep = ctx.enter_context(tc.tile_pool(name="keep", bufs=1))
+        psum = ctx.enter_context(tc.psum_pool(name="psum", bufs=1))
+
+        def tile(shape, dtype, name, tag=None):
+            return keep.tile(shape, dtype, name=name, tag=tag or name, align_bytes=64)
+
+        def load_list(src, name):
+            dst = tile(list(src.shape), U16, name)
+            nc.sync.dma_start(dst[:], src)
+            return dst
+
+        def zeroed_plane(width, name, engine):
+            plane = tile([P, width], U8, name)
+            engine.memset(plane[:].bitcast(I32), 0)
+            return plane
+
+        def load_scale_rows(plane, src):
+            for q in range(4):
+                nc.sync.dma_start(plane[32 * q : 32 * q + 4, :].bitcast(I32), src[0, 4 * q : 4 * q + 4, :].bitcast(I32))
+
+        def load_weight_words(src, name):
+            dst = tile([P, 2 * H], U8, name)
+            nc.sync.dma_start(dst[:].bitcast(I32), src[0].bitcast(I32))
+            return dst
+
+        def deal(raw, name):
+            dst = tile(list(raw.shape), U8, name)
+            nc.vector.tensor_copy(
+                dst[:].bitcast(I32).rearrange("p (t b e) -> p b t e", t=PACK, b=BLOCKS),
+                raw[:].bitcast(I32).rearrange("p (b t e) -> p b t e", t=PACK, b=BLOCKS),
+            )
+            return dst
+
+        def interleave(copy, planes, name):
+            width = planes.shape[2]
+            grouped = tile([P, width, PACK], BF16, name)
+            copy(grouped[:].rearrange("p (c i) t -> p c t i", i=4), planes.rearrange("p t (c i) -> p c t i", i=4))
+            return grouped
+
+        def quantize(words, scales, grouped):
+            nc.vector.quantize_mx(out=words.bitcast(FP8X4), scales=scales, in_=grouped[:].rearrange("p c t -> p (c t)"))
+
+        def offsets(lst, lo, hi):
+            return lst[:, lo // 16 : hi // 16]
+
+        xs = zeroed_plane(T, "xs", nc.gpsimd)
+        w1s_raw = zeroed_plane(H, "w1s_raw", nc.vector)
+        w2s_raw = zeroed_plane(H, "w2s_raw", nc.vector)
+        gain_rows = tile([P, P], F32, "gain_rows")
+        nc.vector.memset(gain_rows[:], 0.0)
+
+        warm_out = tile([P, 1], F32, "warm_out")
+        nc.scalar.activation(warm_out[:], gain_rows[:, 0:1], ACT.Sigmoid)
+        identity = tile([P, P], F32, "identity")
+        make_identity(nc, identity[:])
+
+        l_offs = load_list(offs, "l_offs")
+        l_two = load_list(two, "l_two")
+        load_scale_rows(xs, x_scales)
+        xw = tile([P, T], I32, "xw")
+        nc.sync.dma_start(xw[:], x_words[0].rearrange("p c r -> p (c r)").bitcast(I32))
+        w1w_raw = load_weight_words(w1_words, "w1w_raw")
+        load_scale_rows(w1s_raw, w1_scales)
+        l1 = load_list(n1, "l1")
+        l2 = load_list(n2, "l2")
+        w2w_raw = load_weight_words(w2_words, "w2w_raw")
+        for j, gain in enumerate((ga, gb)):
+            nc.sync.dma_start(
+                gain_rows[PACK * j : PACK * (j + 1), :].rearrange("t (b r) -> t b r", b=BLOCKS),
+                gain.rearrange("(b t r) o -> t b (r o)", b=BLOCKS, t=PACK),
+            )
+        load_scale_rows(w2s_raw, w2_scales)
+        l4 = load_list(n4, "l4")
+        l3 = load_list(n3, "l3")
+        l5 = load_list(n5, "l5")
+        l6 = load_list(n6, "l6")
+        l7 = load_list(n7, "l7")
+
+        xb_s = tile([P, V], U8, "xb_s")
+        xa_s = tile([P, S], U8, "xa_s")
+        xa_w = tile([P, S], U32, "xa_w")
+        nc.vector.tensor_copy(xa_s[:], xs[:].indirect(l_offs[:]))
+        nc.vector.tensor_copy(xb_s[:], xs[:].indirect(l_two[:]))
+        nc.vector.tensor_copy(xa_w[:], xw[:].bitcast(U32).indirect(l_offs[:]))
+        w1w = deal(w1w_raw, "w1w")
+        w1s = deal(w1s_raw, "w1s")
+        xb_w = tile([P, V], U32, "xb_w", tag="w1s_raw")
+        nc.vector.tensor_copy(xb_w[:], xw[:].bitcast(U32).indirect(l_two[:]))
+        w2w = deal(w2w_raw, "w2w")
+        w2s = deal(w2s_raw, "w2s")
+
+        def project(bank, ww, ws, t, xw_g, xs_g):
+            nc.tensor.matmul_mx(
+                out=bank[:],
+                lhsT=ww[:, 2 * P * t : 2 * P * (t + 1)].bitcast(FP4X4),
+                lhsT_scale=ws[:, P * t : P * (t + 1)],
+                rhs=xw_g[:].bitcast(FP8X4),
+                rhs_scale=xs_g[:],
+                start=True,
+                stop=True,
+            )
+
+        a_ps = [psum.tile([P, S], F32, name=f"a_ps{t}", tag=f"bank{t}") for t in range(PACK)]
+        a_sb = [tile([P, S], F32, f"a_sb{t}") for t in range(PACK)]
+        for t in range(PACK):
+            project(a_ps[t], w1w, w1s, t, xa_w, xa_s)
+            nc.scalar.copy(a_sb[t][:], a_ps[t][:])
+
+        gains_ps = psum.tile([P, V], F32, name="gains_ps", tag="bank7")
+        gains = tile([P, 2 * PACK], F32, "gains")
+        nc.tensor.transpose(gains_ps[:, :P], gain_rows[:], identity[:])
+        nc.scalar.copy(gains[:], gains_ps[:, : 2 * PACK])
+
+        b_ps = [psum.tile([P, V], F32, name=f"b_ps{t}", tag=f"bank{PACK + t}") for t in range(PACK)]
+        b_sb = [tile([P, V], F32, f"b_sb{t}") for t in range(PACK)]
+
+        z_planes = tile([P, PACK, S], BF16, "z_planes")
+        pa = [tile([P, W], F32, f"pa{t}") for t in range(PACK)]
+        diff = [tile([P, W], F32, f"diff{t}") for t in range(PACK)]
+        up = [tile([P, W], F32, f"up{t}") for t in range(PACK)]
+        down_abs = [tile([P, W], F32, f"down_abs{t}") for t in range(PACK)]
+        down = [tile([P, W], F32, f"down{t}") for t in range(PACK)]
+        dt = [tile([P, S], F32, f"dt{t}") for t in range(PACK)]
+        for step in range(PACK + 1):
+            if step < PACK:
+                nc.vector.tensor_copy(pa[step][:], a_sb[step][:].indirect(l1[:]))
+            if 1 <= step:
+                t = step - 1
+                nc.vector.tensor_tensor(dt[t][:].indirect(l1[:]), pa[t][:], up[t][:], ALU.add)
+            if step < PACK:
+                t = step
+                nc.vector.tensor_tensor(diff[t][:], a_sb[t][:].indirect(l2[:]), pa[t][:], ALU.subtract)
+                nc.scalar.activation(up[t][:], diff[t][:], ACT.Relu)
+                nc.scalar.activation(down_abs[t][:], diff[t][:], ACT.Relu, scale=-1.0)
+                nc.scalar.activation(down[t][:], down_abs[t][:], ACT.Copy, scale=-1.0)
+                project(b_ps[t], w2w, w2s, t, xb_w, xb_s)
+                nc.scalar.copy(b_sb[t][:], b_ps[t][:])
+            if 1 <= step:
+                t = step - 1
+                nc.vector.tensor_tensor(dt[t][:].indirect(l2[:]), pa[t][:], down[t][:], ALU.add)
+                nc.scalar.activation(
+                    z_planes[:, t, :].rearrange("p (u m) -> p m u", u=PACK),
+                    dt[t][:].rearrange("p (m u) -> p m u", u=PACK),
+                    ACT.Copy,
+                    scale=gains[:, t : t + 1],
+                )
+
+        z_grouped = interleave(nc.scalar.copy, z_planes[:], "z_grouped")
+        z_w = tile([P, S], U32, "z_w")
+        z_s = tile([P, S], U8, "z_s")
+
+        s_ps = [psum.tile([P, V], F32, name=f"s_ps{u}", tag=f"bank{u}") for u in range(PACK)]
+        s_sb = [tile([P, V], F32, f"s_sb{u}") for u in range(PACK)]
+        sig_low = [tile([P, HALF], F32, f"sig_low{u}") for u in range(PACK)]
+
+        def scores(c, grouped):
+            lo, hi = CHUNKS[c]
+            z2_w = tile([P, hi - lo], U32, f"z2_w{c}")
+            z2_s = tile([P, hi - lo], U8, f"z2_s{c}")
+            quantize(z2_w[:], z2_s[:], grouped)
+            for u in range(PACK):
+                nc.tensor.matmul_mx(
+                    out=s_ps[u][:, lo:hi],
+                    lhsT=z_w[:, P * u : P * (u + 1)].bitcast(FP8X4),
+                    lhsT_scale=z_s[:, P * u : P * (u + 1)],
+                    rhs=z2_w[:].bitcast(FP8X4),
+                    rhs_scale=z2_s[:],
+                    start=True,
+                    stop=True,
+                )
+                if c == 0 or u == 0:
+                    nc.scalar.activation(s_sb[u][:, lo:hi], s_ps[u][:, lo:hi], ACT.Copy, scale=0.0625)
+                if c == 0:
+                    nc.scalar.activation(sig_low[u][:], s_ps[u][:, lo:hi], ACT.Sigmoid, scale=0.0625)
+
+        units = [(c, t) for c in range(len(CHUNKS)) for t in range(PACK)]
+        z2_planes = [tile([P, PACK, hi - lo], BF16, f"z2_planes{lo}") for lo, hi in CHUNKS]
+        b4 = {}
+        bd = {}
+        pending = []
+        for step in range(len(units) + 2):
+            if step < len(units):
+                c, t = units[step]
+                lo, hi = CHUNKS[c]
+                b4[step] = tile([P, hi - lo], F32, f"b4_{step}")
+                nc.vector.tensor_copy(b4[step][:], b_sb[t][:].indirect(offsets(l4, lo, hi)))
+            if 2 <= step:
+                c, t = units[step - 2]
+                lo, hi = CHUNKS[c]
+                nc.vector.scalar_tensor_tensor(
+                    z2_planes[c][:, t, :], bd[step - 2][:], gains[:, PACK + t : PACK + t + 1], b_ps[t][:, lo:hi], ALU.mult, ALU.mult
+                )
+                if t == PACK - 1:
+                    copy = nc.vector.tensor_copy if c == len(CHUNKS) - 1 else nc.scalar.copy
+                    pending.append((c, interleave(copy, z2_planes[c][:], f"z2_grouped{c}")))
+            if 1 <= step <= len(units):
+                c, t = units[step - 1]
+                lo, hi = CHUNKS[c]
+                bd[step - 1] = tile([P, hi - lo], F32, f"bd_{step}")
+                nc.vector.tensor_tensor(bd[step - 1][:], b_sb[t][:].indirect(offsets(l3, lo, hi)), b4[step - 1][:], ALU.subtract)
+            if step == 3:
+                quantize(z_w[:], z_s[:], z_grouped)
+            if step in (8, 11, len(units) + 1):
+                scores(*pending.pop())
+
+
+        y_w = tile([P, V], I32, "y_w")
+        y_s = tile([P, V], U8, "y_s")
+        out_rows = out_0.rearrange("(p u) v -> p u v", u=PACK)
+        out_words = out_1[0].rearrange("p c r -> p (c r)").bitcast(I32)
+        y_low = tile([P, PACK, HALF], F32, "y_low")
+        y_high = tile([P, 2, PACK, QUARTER], F32, "y_high")
+        units = [(u, 0, HALF) for u in range(PACK)] + [(u, HALF, V) for u in range(PACK - 1)]
+        units = units + [(PACK - 1, HALF, HALF + QUARTER), (PACK - 1, HALF + QUARTER, V)]
+        first = {}
+        second = {}
+        y_grouped = {}
+        for step in range(len(units) + 1):
+            if step < len(units):
+                u, lo, hi = units[step]
+                if lo == 0:
+                    sig = sig_low[u]
+                    if u > 0:
+                        nc.scalar.activation(s_sb[u][:, HALF:], s_ps[u][:, HALF:], ACT.Copy, scale=0.0625)
+                else:
+                    sig = tile([P, hi - lo], F32, f"sig{step}")
+                    nc.scalar.activation(sig[:], s_ps[u][:, lo:hi], ACT.Sigmoid, scale=0.0625)
+                sig7 = tile([P, hi - lo], F32, f"sig7_{step}")
+                nc.scalar.activation(sig7[:], s_sb[u][:].indirect(offsets(l7, lo, hi)), ACT.Sigmoid)
+                first[step] = tile([P, hi - lo], F32, f"first{step}")
+                second[step] = tile([P, hi - lo], F32, f"second{step}")
+                nc.vector.tensor_tensor(first[step][:], s_sb[u][:].indirect(offsets(l5, lo, hi)), sig[:], ALU.mult)
+            if 1 <= step:
+                pu, plo, phi = units[step - 1]
+                if plo == 0:
+                    nc.vector.tensor_tensor(y_low[:, pu, :], first[step - 1][:], second[step - 1][:], ALU.add)
+                    nc.sync.dma_start(out_rows[:, pu, :HALF], y_low[:, pu, :])
+                else:
+                    parts = slice((plo - HALF) // QUARTER, (phi - HALF) // QUARTER)
+                    nc.vector.tensor_tensor(
+                        y_high[:, parts, pu, :],
+                        first[step - 1][:].rearrange("p (a c) -> p a c", c=QUARTER),
+                        second[step - 1][:].rearrange("p (a c) -> p a c", c=QUARTER),
+                        ALU.add,
+                    )
+                    if phi == V:
+                        nc.sync.dma_start(out_rows[:, pu, HALF:].rearrange("p (a c) -> p a c", c=QUARTER), y_high[:, :, pu, :])
+                if step == PACK:
+                    y_grouped[0] = interleave(nc.scalar.copy, y_low[:], "y_grouped0")
+                if step == len(units) - 1:
+                    y_grouped[1] = interleave(nc.scalar.copy, y_high[:, 0], "y_grouped1")
+                if step == len(units):
+                    y_grouped[2] = interleave(nc.vector.tensor_copy, y_high[:, 1], "y_grouped2")
+                    quantize(y_w[:, HALF : HALF + QUARTER], y_s[:, HALF : HALF + QUARTER], y_grouped[1])
+                    quantize(y_w[:, HALF + QUARTER :], y_s[:, HALF + QUARTER :], y_grouped[2])
+                    nc.sync.dma_start(out_words[:, HALF:], y_w[:, HALF:])
+            if step < len(units):
+                nc.vector.tensor_tensor(second[step][:], s_sb[u][:].indirect(offsets(l6, lo, hi)), sig7[:], ALU.mult)
+            if step == PACK + 1:
+                quantize(y_w[:, :HALF], y_s[:, :HALF], y_grouped[0])
+                nc.sync.dma_start(out_words[:, :HALF], y_w[:, :HALF])
+        for q in range(4):
+            queue = nc.sync if q % 2 else nc.scalar
+            queue.dma_start(out_2[0, 4 * q : 4 * q + 4, :].bitcast(I32), y_s[32 * q : 32 * q + 4, :].bitcast(I32))

@@ -22,7 +22,7 @@ PACK = 4
 HALF = 256
 QUARTER = 128
 BLOCKS = 16
-CHUNKS = ((0, 256), (256, 384), (384, 512))
+EARLY = 384
 
 
 def tile_picked_kqorderwindwsum_none_po_kernel(tc, x_words, x_scales, w1_words, w1_scales, w2_words, w2_scales, ga, gb, offs, two, n1, n2, n3, n4, n5, n6, n7, out_0, out_1, out_2):
@@ -44,17 +44,17 @@ def tile_picked_kqorderwindwsum_none_po_kernel(tc, x_words, x_scales, w1_words, 
             engine.memset(plane[:].bitcast(I32), 0)
             return plane
 
-        def load_scale_rows(plane, src):
+        def load_scale_rows(plane, src, queues=(nc.sync, nc.sync)):
             for q in range(4):
-                nc.sync.dma_start(plane[32 * q : 32 * q + 4, :].bitcast(I32), src[0, 4 * q : 4 * q + 4, :].bitcast(I32))
+                queues[q % 2].dma_start(plane[32 * q : 32 * q + 4, :].bitcast(I32), src[0, 4 * q : 4 * q + 4, :].bitcast(I32))
 
         def load_weight_words(src, name):
             dst = tile([P, 2 * H], U8, name)
             nc.sync.dma_start(dst[:].bitcast(I32), src[0].bitcast(I32))
             return dst
 
-        def deal(raw, name):
-            dst = tile(list(raw.shape), U8, name)
+        def deal(raw, name, tag=None):
+            dst = tile(list(raw.shape), U8, name, tag)
             nc.vector.tensor_copy(
                 dst[:].bitcast(I32).rearrange("p (t b e) -> p b t e", t=PACK, b=BLOCKS),
                 raw[:].bitcast(I32).rearrange("p (b t e) -> p b t e", t=PACK, b=BLOCKS),
@@ -68,7 +68,7 @@ def tile_picked_kqorderwindwsum_none_po_kernel(tc, x_words, x_scales, w1_words, 
             return grouped
 
         def quantize(words, scales, grouped):
-            nc.vector.quantize_mx(out=words.bitcast(FP8X4), scales=scales, in_=grouped[:].rearrange("p c t -> p (c t)"))
+            nc.vector.quantize_mx(out=words.bitcast(FP8X4), scales=scales, in_=grouped.rearrange("p c t -> p (c t)"))
 
         def offsets(lst, lo, hi):
             return lst[:, lo // 16 : hi // 16]
@@ -79,27 +79,29 @@ def tile_picked_kqorderwindwsum_none_po_kernel(tc, x_words, x_scales, w1_words, 
         gain_rows = tile([P, P], F32, "gain_rows")
         nc.vector.memset(gain_rows[:], 0.0)
 
-        warm_out = tile([P, 1], F32, "warm_out")
-        nc.scalar.activation(warm_out[:], gain_rows[:, 0:1], ACT.Sigmoid)
         identity = tile([P, P], F32, "identity")
         make_identity(nc, identity[:])
+        warm_out = tile([P, 1], F32, "warm_out")
+        nc.scalar.activation(warm_out[:], identity[:, 0:1], ACT.Sigmoid)
 
-        l_offs = load_list(offs, "l_offs")
-        l_two = load_list(two, "l_two")
-        load_scale_rows(xs, x_scales)
         xw = tile([P, T], I32, "xw")
-        nc.sync.dma_start(xw[:], x_words[0].rearrange("p c r -> p (c r)").bitcast(I32))
+        x_view = x_words[0].rearrange("p c r -> p (c r)").bitcast(I32)
+        nc.sync.dma_start(xw[:, :512], x_view[:, :512])
+        l_offs = load_list(offs, "l_offs")
+        load_scale_rows(xs, x_scales, (nc.sync, nc.scalar))
+        l_two = load_list(two, "l_two")
+        nc.sync.dma_start(xw[:, 512:], x_view[:, 512:])
         w1w_raw = load_weight_words(w1_words, "w1w_raw")
         load_scale_rows(w1s_raw, w1_scales)
         l1 = load_list(n1, "l1")
         l2 = load_list(n2, "l2")
         w2w_raw = load_weight_words(w2_words, "w2w_raw")
+        load_scale_rows(w2s_raw, w2_scales)
         for j, gain in enumerate((ga, gb)):
             nc.sync.dma_start(
                 gain_rows[PACK * j : PACK * (j + 1), :].rearrange("t (b r) -> t b r", b=BLOCKS),
                 gain.rearrange("(b t r) o -> t b (r o)", b=BLOCKS, t=PACK),
             )
-        load_scale_rows(w2s_raw, w2_scales)
         l4 = load_list(n4, "l4")
         l3 = load_list(n3, "l3")
         l5 = load_list(n5, "l5")
@@ -117,7 +119,6 @@ def tile_picked_kqorderwindwsum_none_po_kernel(tc, x_words, x_scales, w1_words, 
         xb_w = tile([P, V], U32, "xb_w", tag="w1s_raw")
         nc.vector.tensor_copy(xb_w[:], xw[:].bitcast(U32).indirect(l_two[:]))
         w2w = deal(w2w_raw, "w2w")
-        w2s = deal(w2s_raw, "w2s")
 
         def project(bank, ww, ws, t, xw_g, xs_g):
             nc.tensor.matmul_mx(
@@ -136,159 +137,264 @@ def tile_picked_kqorderwindwsum_none_po_kernel(tc, x_words, x_scales, w1_words, 
             project(a_ps[t], w1w, w1s, t, xa_w, xa_s)
             nc.scalar.copy(a_sb[t][:], a_ps[t][:])
 
-        gains_ps = psum.tile([P, V], F32, name="gains_ps", tag="bank7")
+        gains_ps = psum.tile([P, V], F32, name="gains_ps", tag="bank0")
         gains = tile([P, 2 * PACK], F32, "gains")
         nc.tensor.transpose(gains_ps[:, :P], gain_rows[:], identity[:])
         nc.scalar.copy(gains[:], gains_ps[:, : 2 * PACK])
+        gb_neg = tile([P, PACK], F32, "gb_neg")
+        nc.scalar.activation(gb_neg[:], gains_ps[:, PACK : 2 * PACK], ACT.Copy, scale=-1.0)
 
         b_ps = [psum.tile([P, V], F32, name=f"b_ps{t}", tag=f"bank{PACK + t}") for t in range(PACK)]
-        b_sb = [tile([P, V], F32, f"b_sb{t}") for t in range(PACK)]
+        b_sb = [tile([P, 2 * V], F32, f"b_sb{t}") for t in range(PACK)]
+        b_late = [tile([P, V], F32, f"b_late{t}") for t in range(PACK)]
+        pe_cols = EARLY
+        b_pos = [tile([P, pe_cols], F32, f"b_pos{t}") for t in range(PACK)]
+        b_neg = [tile([P, pe_cols], F32, f"b_neg{t}") for t in range(PACK)]
 
-        z_planes = tile([P, PACK, S], BF16, "z_planes")
-        pa = [tile([P, W], F32, f"pa{t}") for t in range(PACK)]
-        diff = [tile([P, W], F32, f"diff{t}") for t in range(PACK)]
-        up = [tile([P, W], F32, f"up{t}") for t in range(PACK)]
-        down_abs = [tile([P, W], F32, f"down_abs{t}") for t in range(PACK)]
-        down = [tile([P, W], F32, f"down{t}") for t in range(PACK)]
-        dt = [tile([P, S], F32, f"dt{t}") for t in range(PACK)]
-        for step in range(PACK + 1):
-            if step < PACK:
-                nc.vector.tensor_copy(pa[step][:], a_sb[step][:].indirect(l1[:]))
-            if 1 <= step:
-                t = step - 1
-                nc.vector.tensor_tensor(dt[t][:].indirect(l1[:]), pa[t][:], up[t][:], ALU.add)
-            if step < PACK:
-                t = step
-                nc.vector.tensor_tensor(diff[t][:], a_sb[t][:].indirect(l2[:]), pa[t][:], ALU.subtract)
-                nc.scalar.activation(up[t][:], diff[t][:], ACT.Relu)
-                nc.scalar.activation(down_abs[t][:], diff[t][:], ACT.Relu, scale=-1.0)
-                nc.scalar.activation(down[t][:], down_abs[t][:], ACT.Copy, scale=-1.0)
-                project(b_ps[t], w2w, w2s, t, xb_w, xb_s)
-                nc.scalar.copy(b_sb[t][:], b_ps[t][:])
-            if 1 <= step:
-                t = step - 1
-                nc.vector.tensor_tensor(dt[t][:].indirect(l2[:]), pa[t][:], down[t][:], ALU.add)
-                nc.scalar.activation(
-                    z_planes[:, t, :].rearrange("p (u m) -> p m u", u=PACK),
-                    dt[t][:].rearrange("p (m u) -> p m u", u=PACK),
-                    ACT.Copy,
-                    scale=gains[:, t : t + 1],
-                )
+        z_grouped = [tile([P, P, PACK], BF16, f"z_grouped{u}") for u in range(PACK)]
+        pa, diff, up, down, dt = {}, {}, {}, {}, {}
 
-        z_grouped = interleave(nc.scalar.copy, z_planes[:], "z_grouped")
-        z_w = tile([P, S], U32, "z_w")
-        z_s = tile([P, S], U8, "z_s")
+        def fetch_first(t):
+            pa[t] = tile([P, W], F32, f"pa{t}", (None, None, "diff0", "diff1")[t])
+            nc.vector.tensor_copy(pa[t][:], a_sb[t][:].indirect(l1[:]))
 
-        s_ps = [psum.tile([P, V], F32, name=f"s_ps{u}", tag=f"bank{u}") for u in range(PACK)]
-        s_sb = [tile([P, V], F32, f"s_sb{u}") for u in range(PACK)]
-        sig_low = [tile([P, HALF], F32, f"sig_low{u}") for u in range(PACK)]
+        def fetch_difference(t):
+            diff[t] = tile([P, W], F32, f"diff{t}", (None, None, "up0", "up1")[t])
+            nc.vector.tensor_tensor(diff[t][:], a_sb[t][:].indirect(l2[:]), pa[t][:], ALU.subtract)
+            down_abs = tile([P, W], F32, f"down_abs{t}")
+            down[t] = tile([P, W], F32, f"down{t}")
+            up[t] = tile([P, W], F32, f"up{t}")
+            nc.scalar.activation(down_abs[:], diff[t][:], ACT.Relu, scale=-1.0)
+            nc.scalar.activation(down[t][:], down_abs[:], ACT.Copy, scale=-1.0)
+            nc.scalar.activation(up[t][:], diff[t][:], ACT.Relu)
 
-        def scores(c, grouped):
-            lo, hi = CHUNKS[c]
-            z2_w = tile([P, hi - lo], U32, f"z2_w{c}")
-            z2_s = tile([P, hi - lo], U8, f"z2_s{c}")
-            quantize(z2_w[:], z2_s[:], grouped)
+        def put_larger(t):
+            dt[t] = tile([P, S], F32, f"dt{t}", (None, None, None, "pairs0")[t])
+            nc.vector.tensor_tensor(dt[t][:].indirect(l1[:]), pa[t][:], up[t][:], ALU.add)
+
+        def put_smaller(t):
+            nc.vector.tensor_tensor(dt[t][:].indirect(l2[:]), pa[t][:], down[t][:], ALU.add)
             for u in range(PACK):
-                nc.tensor.matmul_mx(
-                    out=s_ps[u][:, lo:hi],
-                    lhsT=z_w[:, P * u : P * (u + 1)].bitcast(FP8X4),
-                    lhsT_scale=z_s[:, P * u : P * (u + 1)],
-                    rhs=z2_w[:].bitcast(FP8X4),
-                    rhs_scale=z2_s[:],
-                    start=True,
-                    stop=True,
-                )
-                if c == 0 or u == 0:
-                    nc.scalar.activation(s_sb[u][:, lo:hi], s_ps[u][:, lo:hi], ACT.Copy, scale=0.0625)
-                if c == 0:
-                    nc.scalar.activation(sig_low[u][:], s_ps[u][:, lo:hi], ACT.Sigmoid, scale=0.0625)
+                nc.scalar.activation(z_grouped[u][:, :, t], dt[t][:, u::PACK], ACT.Copy, scale=gains[:, t : t + 1])
 
-        units = [(c, t) for c in range(len(CHUNKS)) for t in range(PACK)]
-        z2_planes = [tile([P, PACK, hi - lo], BF16, f"z2_planes{lo}") for lo, hi in CHUNKS]
-        b4 = {}
-        bd = {}
-        pending = []
-        for step in range(len(units) + 2):
-            if step < len(units):
-                c, t = units[step]
-                lo, hi = CHUNKS[c]
-                b4[step] = tile([P, hi - lo], F32, f"b4_{step}")
-                nc.vector.tensor_copy(b4[step][:], b_sb[t][:].indirect(offsets(l4, lo, hi)))
-            if 2 <= step:
-                c, t = units[step - 2]
-                lo, hi = CHUNKS[c]
-                nc.vector.scalar_tensor_tensor(
-                    z2_planes[c][:, t, :], bd[step - 2][:], gains[:, PACK + t : PACK + t + 1], b_ps[t][:, lo:hi], ALU.mult, ALU.mult
+        def second_projection(t):
+            project(b_ps[t], w2w, w2s, t, xb_w, xb_s)
+            nc.scalar.copy(b_sb[t][:, :V], b_ps[t][:])
+            nc.scalar.activation(b_pos[t][:], b_ps[t][:, :pe_cols], ACT.Copy, scale=gains[:, PACK + t : PACK + t + 1])
+            nc.scalar.activation(b_neg[t][:], b_ps[t][:, :pe_cols], ACT.Copy, scale=gb_neg[:, t : t + 1])
+            nc.sync.dma_start(b_late[t][:], b_sb[t][:, :V])
+
+        last_term = []
+
+        def fetch_term(t, sign):
+            term = tile([P, EARLY], F32, f"term{t}_{sign}")
+            lst, factor = ((l3, b_pos), (l4, b_neg))[sign]
+            nc.vector.tensor_tensor(term[:], b_sb[t][:].indirect(offsets(lst, 0, EARLY)), factor[t][:], ALU.mult)
+            last_term.append(term)
+            return term
+
+        def turn(t, plus, minus):
+            for j in range(EARLY // P):
+                cols = slice(P * j, P * (j + 1))
+                nc.tensor.matmul(turned[j][:, t, :], plus[:, cols], identity[:], is_transpose=True, start=True, stop=False)
+                nc.tensor.matmul(turned[j][:, t, :], minus[:, cols], identity[:], is_transpose=True, start=False, stop=True)
+
+        def turn_back():
+            grouped = tile([P, EARLY, PACK], BF16, "z2_early")
+            pairs = [tile([P, 2, P, 2], BF16, f"pairs{j}") for j in range(EARLY // P)]
+            for j in range(EARLY // P):
+                nc.scalar.copy(pairs[j][:], turned[j][:].rearrange("v (w e) p -> v w p e", e=2))
+            for j in range(EARLY // P):
+                words = pairs[j][:].rearrange("v w p e -> v (w p e)").bitcast(F32)
+                back = psum.tile([P, 2, P], F32, name=f"back{j}", tag=f"bank{PACK + j}")
+                for w in range(2):
+                    nc.tensor.transpose(back[:, w, :], words[:, P * w : P * (w + 1)], identity[:])
+                nc.scalar.copy(
+                    grouped[:, P * j : P * (j + 1), :].rearrange("p v t -> p (v t)").bitcast(F32).rearrange("p (v w) -> p v w", w=2),
+                    back[:].rearrange("p w v -> p v w"),
                 )
-                if t == PACK - 1:
-                    copy = nc.vector.tensor_copy if c == len(CHUNKS) - 1 else nc.scalar.copy
-                    pending.append((c, interleave(copy, z2_planes[c][:], f"z2_grouped{c}")))
-            if 1 <= step <= len(units):
-                c, t = units[step - 1]
-                lo, hi = CHUNKS[c]
-                bd[step - 1] = tile([P, hi - lo], F32, f"bd_{step}")
-                nc.vector.tensor_tensor(bd[step - 1][:], b_sb[t][:].indirect(offsets(l3, lo, hi)), b4[step - 1][:], ALU.subtract)
-            if step == 3:
-                quantize(z_w[:], z_s[:], z_grouped)
-            if step in (8, 11, len(units) + 1):
-                scores(*pending.pop())
+            return grouped
+
+        late4, late_diff = {}, {}
+        z2_planes = tile([P, PACK, V - EARLY], BF16, "z2_planes")
+
+        def fetch_late(t):
+            late4[t] = tile([P, V - EARLY], F32, f"late4_{t}", ("b_pos3", "b_neg3", "term3_0", "term3_1")[t])
+            nc.vector.tensor_copy(late4[t][:], b_late[t][:].indirect(offsets(l4, EARLY, V)))
+
+        def subtract_late(t):
+            late_diff[t] = tile([P, V - EARLY], F32, f"late_diff{t}", (None, "pairs1", "z2_early", "z_grouped0")[t])
+            nc.vector.tensor_tensor(late_diff[t][:], b_late[t][:].indirect(offsets(l3, EARLY, V)), late4[t][:], ALU.subtract)
+
+        def weigh_late(t):
+            nc.vector.scalar_tensor_tensor(
+                z2_planes[:, t, :], late_diff[t][:], gains[:, PACK + t : PACK + t + 1], b_late[t][:, EARLY:], ALU.mult, ALU.mult
+            )
+
+        fetch_first(0)
+        fetch_difference(0)
+        fetch_first(1)
+        w2s = deal(w2s_raw, "w2s", "a_sb0")
+        fetch_difference(1)
+        put_larger(0)
+        fetch_first(2)
+        put_smaller(0)
+        fetch_difference(2)
+        second_projection(0)
+        second_projection(1)
+        put_larger(1)
+        fetch_first(3)
+        put_smaller(1)
+        fetch_difference(3)
+        second_projection(2)
+        second_projection(3)
+        turned = [psum.tile([P, PACK, P], F32, name=f"turned{j}", tag=f"bank{PACK + j}") for j in range(EARLY // P)]
+        put_larger(2)
+        plus = fetch_term(0, 0)
+        put_smaller(2)
+        turn(0, plus, fetch_term(0, 1))
+        for t in range(1, PACK):
+            turn(t, fetch_term(t, 0), fetch_term(t, 1))
+
+        z2_early = turn_back()
+        for t in range(PACK):
+            fetch_late(t)
+        subtract_late(0)
+        put_larger(3)
+        subtract_late(1)
+        put_smaller(3)
+
+
+        z2_w = tile([P, V], U32, "z2_w")
+        z2_s = tile([P, V], U8, "z2_s")
+        z_w = [tile([P, P], U32, f"z_w{u}") for u in range(PACK)]
+        z_s = [tile([P, P], U8, f"z_s{u}") for u in range(PACK)]
+        s_ps = [psum.tile([P, V], F32, name=f"s_ps{u}", tag=f"bank{u}") for u in range(PACK)]
+        s_sb = [tile([P, 2 * V if u < 3 else V], F32, f"s_sb{u}") for u in range(PACK)]
+        sig = [tile([P, V], F32, f"sig{u}") for u in range(PACK)]
+
+        def leave_psum(u, lo, hi):
+            nc.scalar.activation(s_sb[u][:, lo:hi], s_ps[u][:, lo:hi], ACT.Copy, scale=0.0625)
+
+        def own_sigmoid(u, lo, hi):
+            nc.scalar.activation(sig[u][:, lo:hi], s_ps[u][:, lo:hi], ACT.Sigmoid, scale=0.0625)
+
+        def scores(u, lo, hi):
+            nc.tensor.matmul_mx(
+                out=s_ps[u][:, lo:hi],
+                lhsT=z_w[u][:].bitcast(FP8X4),
+                lhsT_scale=z_s[u][:],
+                rhs=z2_w[:, lo:hi].bitcast(FP8X4),
+                rhs_scale=z2_s[:, lo:hi],
+                start=True,
+                stop=True,
+            )
+
+        for lo, hi in ((0, HALF), (HALF, EARLY)):
+            quantize(z2_w[:, lo:hi], z2_s[:, lo:hi], z2_early[:, lo:hi, :])
+        def early_scores(u):
+            for lo, hi in ((0, HALF), (HALF, EARLY)):
+                scores(u, lo, hi)
+            leave_psum(u, 0, EARLY)
+            own_sigmoid(u, 0, EARLY)
+
+        subtract_late(2)
+        weigh_late(0)
+        weigh_late(1)
+        quantize(z_w[0][:], z_s[0][:], z_grouped[0][:])
+        early_scores(0)
+        subtract_late(3)
+        quantize(z_w[1][:], z_s[1][:], z_grouped[1][:])
+        early_scores(1)
+        weigh_late(2)
+        weigh_late(3)
+        quantize(z_w[2][:], z_s[2][:], z_grouped[2][:])
+        z2_late = interleave(nc.vector.tensor_copy, z2_planes[:], "z2_late")
+        quantize(z_w[3][:], z_s[3][:], z_grouped[3][:])
+        quantize(z2_w[:, EARLY:], z2_s[:, EARLY:], z2_late[:])
+        scores(0, EARLY, V)
+        leave_psum(0, EARLY, V)
+        own_sigmoid(0, EARLY, V)
+        scores(1, EARLY, V)
+        for u in range(2, PACK):
+            scores(u, 0, V)
 
 
         y_w = tile([P, V], I32, "y_w")
         y_s = tile([P, V], U8, "y_s")
-        out_rows = out_0.rearrange("(p u) v -> p u v", u=PACK)
+        out_rows = out_0.rearrange("(p u) (g c) -> p u g c", u=PACK, c=QUARTER)
         out_words = out_1[0].rearrange("p c r -> p (c r)").bitcast(I32)
-        y_low = tile([P, PACK, HALF], F32, "y_low")
-        y_high = tile([P, 2, PACK, QUARTER], F32, "y_high")
-        units = [(u, 0, HALF) for u in range(PACK)] + [(u, HALF, V) for u in range(PACK - 1)]
-        units = units + [(PACK - 1, HALF, HALF + QUARTER), (PACK - 1, HALF + QUARTER, V)]
+        y = tile([P, PACK, PACK, QUARTER], F32, "y")
+        units = [(0, 0, V), (1, 0, V), (2, 0, V), (3, 0, HALF), (3, HALF, HALF + QUARTER), (3, HALF + QUARTER, V)]
+
+        def regroup(copy, lo, hi):
+            grouped_y = tile([P, hi - lo, PACK], BF16, f"y_grouped{lo}")
+            for g in range(lo // QUARTER, hi // QUARTER):
+                copy(
+                    grouped_y[:, QUARTER * g - lo : QUARTER * (g + 1) - lo, :].rearrange("p (c i) u -> p c u i", i=4),
+                    y[:, g].rearrange("p u (c i) -> p c u i", i=4),
+                )
+            return grouped_y
+
+        def add_turned():
+            sums = {}
+            for k in range(2):
+                sum_ps = psum.tile([P, PACK, P], F32, name=f"sum_ps{k}", tag=f"bank{PACK + k}")
+                for g in range(PACK):
+                    cols = slice(P * g, P * (g + 1))
+                    nc.tensor.matmul(sum_ps[:, g, :], first[k][:, cols], identity[:], is_transpose=True, start=True, stop=False)
+                    nc.tensor.matmul(sum_ps[:, g, :], second[k][:, cols], identity[:], is_transpose=True, start=False, stop=True)
+                sums[k] = tile([P, PACK, P], F32, f"sums{k}")
+                nc.scalar.copy(sums[k][:], sum_ps[:])
+            for k in range(2):
+                y_ps = psum.tile([P, PACK, P], F32, name=f"y_ps{k}", tag=f"bank{PACK + 2 + k}")
+                for g in range(PACK):
+                    nc.tensor.transpose(y_ps[:, g, :], sums[k][:, g, :], identity[:])
+                nc.scalar.copy(y[:, :, k, :], y_ps[:])
+                nc.sync.dma_start(out_rows[:, k, :, :], y[:, :, k, :])
+
         first = {}
         second = {}
         y_grouped = {}
         for step in range(len(units) + 1):
             if step < len(units):
                 u, lo, hi = units[step]
-                if lo == 0:
-                    sig = sig_low[u]
-                    if u > 0:
-                        nc.scalar.activation(s_sb[u][:, HALF:], s_ps[u][:, HALF:], ACT.Copy, scale=0.0625)
-                else:
-                    sig = tile([P, hi - lo], F32, f"sig{step}")
-                    nc.scalar.activation(sig[:], s_ps[u][:, lo:hi], ACT.Sigmoid, scale=0.0625)
+                done = EARLY if u == 1 else 0
+                if u > 0 and lo == 0:
+                    leave_psum(u, done, V)
+                if u > 0 and hi > done:
+                    own_sigmoid(u, max(lo, done), hi)
                 sig7 = tile([P, hi - lo], F32, f"sig7_{step}")
                 nc.scalar.activation(sig7[:], s_sb[u][:].indirect(offsets(l7, lo, hi)), ACT.Sigmoid)
                 first[step] = tile([P, hi - lo], F32, f"first{step}")
                 second[step] = tile([P, hi - lo], F32, f"second{step}")
-                nc.vector.tensor_tensor(first[step][:], s_sb[u][:].indirect(offsets(l5, lo, hi)), sig[:], ALU.mult)
+                nc.vector.tensor_tensor(first[step][:], s_sb[u][:].indirect(offsets(l5, lo, hi)), sig[u][:, lo:hi], ALU.mult)
             if 1 <= step:
                 pu, plo, phi = units[step - 1]
-                if plo == 0:
-                    nc.vector.tensor_tensor(y_low[:, pu, :], first[step - 1][:], second[step - 1][:], ALU.add)
-                    nc.sync.dma_start(out_rows[:, pu, :HALF], y_low[:, pu, :])
-                else:
-                    parts = slice((plo - HALF) // QUARTER, (phi - HALF) // QUARTER)
+                groups = slice(plo // QUARTER, phi // QUARTER)
+                if pu >= 2:
                     nc.vector.tensor_tensor(
-                        y_high[:, parts, pu, :],
-                        first[step - 1][:].rearrange("p (a c) -> p a c", c=QUARTER),
-                        second[step - 1][:].rearrange("p (a c) -> p a c", c=QUARTER),
+                        y[:, groups, pu, :],
+                        first[step - 1][:].rearrange("p (g c) -> p g c", c=QUARTER),
+                        second[step - 1][:].rearrange("p (g c) -> p g c", c=QUARTER),
                         ALU.add,
                     )
-                    if phi == V:
-                        nc.sync.dma_start(out_rows[:, pu, HALF:].rearrange("p (a c) -> p a c", c=QUARTER), y_high[:, :, pu, :])
-                if step == PACK:
-                    y_grouped[0] = interleave(nc.scalar.copy, y_low[:], "y_grouped0")
+                    if phi != HALF + QUARTER:
+                        stored = slice(0 if plo == 0 else 2, phi // QUARTER)
+                        nc.sync.dma_start(out_rows[:, pu, stored, :], y[:, stored, pu, :])
                 if step == len(units) - 1:
-                    y_grouped[1] = interleave(nc.scalar.copy, y_high[:, 0], "y_grouped1")
+                    add_turned()
+                    y_grouped[0] = regroup(nc.scalar.copy, 0, HALF)
+                    y_grouped[1] = regroup(nc.scalar.copy, HALF, HALF + QUARTER)
                 if step == len(units):
-                    y_grouped[2] = interleave(nc.vector.tensor_copy, y_high[:, 1], "y_grouped2")
-                    quantize(y_w[:, HALF : HALF + QUARTER], y_s[:, HALF : HALF + QUARTER], y_grouped[1])
-                    quantize(y_w[:, HALF + QUARTER :], y_s[:, HALF + QUARTER :], y_grouped[2])
-                    nc.sync.dma_start(out_words[:, HALF:], y_w[:, HALF:])
+                    y_grouped[2] = regroup(nc.vector.tensor_copy, HALF + QUARTER, V)
+                    quantize(y_w[:, :HALF], y_s[:, :HALF], y_grouped[0][:])
+                    quantize(y_w[:, HALF:EARLY], y_s[:, HALF:EARLY], y_grouped[1][:])
+                    nc.sync.dma_start(out_words[:, :EARLY], y_w[:, :EARLY])
+                    quantize(y_w[:, EARLY:], y_s[:, EARLY:], y_grouped[2][:])
+                    nc.scalar.dma_start(out_words[:, EARLY:], y_w[:, EARLY:])
             if step < len(units):
                 nc.vector.tensor_tensor(second[step][:], s_sb[u][:].indirect(offsets(l6, lo, hi)), sig7[:], ALU.mult)
-            if step == PACK + 1:
-                quantize(y_w[:, :HALF], y_s[:, :HALF], y_grouped[0])
-                nc.sync.dma_start(out_words[:, :HALF], y_w[:, :HALF])
         for q in range(4):
-            queue = nc.sync if q % 2 else nc.scalar
+            queue = nc.scalar if q % 2 else nc.sync
             queue.dma_start(out_2[0, 4 * q : 4 * q + 4, :].bitcast(I32), y_s[32 * q : 32 * q + 4, :].bitcast(I32))

@@ -73,7 +73,9 @@ def tile_picked_kqorderwindwsum_none_po_kernel(tc, x_words, x_scales, w1_words, 
         def offsets(lst, lo, hi):
             return lst[:, lo // 16 : hi // 16]
 
-        xs = zeroed_plane(T, "xs", nc.gpsimd)
+        xs = tile([P, T], U8, "xs")
+        nc.gpsimd.memset(xs[:, : T // 2].bitcast(I32), 0)
+        nc.vector.memset(xs[:, T // 2 :].bitcast(I32), 0)
         w1s_raw = zeroed_plane(H, "w1s_raw", nc.vector)
         w2s_raw = zeroed_plane(H, "w2s_raw", nc.vector)
         gain_rows = tile([P, P], F32, "gain_rows")
@@ -122,19 +124,23 @@ def tile_picked_kqorderwindwsum_none_po_kernel(tc, x_words, x_scales, w1_words, 
 
         def project(bank, ww, ws, t, xw_g, xs_g):
             nc.tensor.matmul_mx(
-                out=bank[:],
+                out=bank,
                 lhsT=ww[:, 2 * P * t : 2 * P * (t + 1)].bitcast(FP4X4),
                 lhsT_scale=ws[:, P * t : P * (t + 1)],
-                rhs=xw_g[:].bitcast(FP8X4),
-                rhs_scale=xs_g[:],
+                rhs=xw_g.bitcast(FP8X4),
+                rhs_scale=xs_g,
                 start=True,
                 stop=True,
             )
 
         a_ps = [psum.tile([P, S], F32, name=f"a_ps{t}", tag=f"bank{t}") for t in range(PACK)]
         a_sb = [tile([P, S], F32, f"a_sb{t}") for t in range(PACK)]
-        for t in range(PACK):
-            project(a_ps[t], w1w, w1s, t, xa_w, xa_s)
+        a_ps_high = psum.tile([P, S], F32, name="a_ps_high", tag="bank7")
+        for bank, cols in ((a_ps[0], slice(0, HALF)), (a_ps_high, slice(HALF, S))):
+            project(bank[:, cols], w1w, w1s, 0, xa_w[:, cols], xa_s[:, cols])
+            nc.scalar.copy(a_sb[0][:, cols], bank[:, cols])
+        for t in range(1, PACK):
+            project(a_ps[t][:], w1w, w1s, t, xa_w[:], xa_s[:])
             nc.scalar.copy(a_sb[t][:], a_ps[t][:])
 
         gains_ps = psum.tile([P, V], F32, name="gains_ps", tag="bank0")
@@ -146,13 +152,12 @@ def tile_picked_kqorderwindwsum_none_po_kernel(tc, x_words, x_scales, w1_words, 
 
         b_ps = [psum.tile([P, V], F32, name=f"b_ps{t}", tag=f"bank{PACK + t}") for t in range(PACK)]
         b_sb = [tile([P, 2 * V], F32, f"b_sb{t}") for t in range(PACK)]
-        b_late = [tile([P, V], F32, f"b_late{t}") for t in range(PACK)]
-        pe_cols = EARLY
+        pe_cols = V
         b_pos = [tile([P, pe_cols], F32, f"b_pos{t}") for t in range(PACK)]
         b_neg = [tile([P, pe_cols], F32, f"b_neg{t}") for t in range(PACK)]
 
         z_grouped = [tile([P, P, PACK], BF16, f"z_grouped{u}") for u in range(PACK)]
-        pa, diff, up, down, dt = {}, {}, {}, {}, {}
+        pa, diff, up, down_abs, down, dt = {}, {}, {}, {}, {}, {}
 
         def fetch_first(t):
             pa[t] = tile([P, W], F32, f"pa{t}", (None, None, "diff0", "diff1")[t])
@@ -161,15 +166,19 @@ def tile_picked_kqorderwindwsum_none_po_kernel(tc, x_words, x_scales, w1_words, 
         def fetch_difference(t):
             diff[t] = tile([P, W], F32, f"diff{t}", (None, None, "up0", "up1")[t])
             nc.vector.tensor_tensor(diff[t][:], a_sb[t][:].indirect(l2[:]), pa[t][:], ALU.subtract)
-            down_abs = tile([P, W], F32, f"down_abs{t}")
-            down[t] = tile([P, W], F32, f"down{t}")
+            down_abs[t] = tile([P, W], F32, f"down_abs{t}")
             up[t] = tile([P, W], F32, f"up{t}")
-            nc.scalar.activation(down_abs[:], diff[t][:], ACT.Relu, scale=-1.0)
-            nc.scalar.activation(down[t][:], down_abs[:], ACT.Copy, scale=-1.0)
+            nc.scalar.activation(down_abs[t][:], diff[t][:], ACT.Relu, scale=-1.0)
+            if t < 2:
+                negate(t)
             nc.scalar.activation(up[t][:], diff[t][:], ACT.Relu)
 
+        def negate(t):
+            down[t] = tile([P, W], F32, f"down{t}", (None, None, "pairs0", "pairs2")[t])
+            nc.scalar.activation(down[t][:], down_abs[t][:], ACT.Copy, scale=-1.0)
+
         def put_larger(t):
-            dt[t] = tile([P, S], F32, f"dt{t}", (None, None, None, "pairs0")[t])
+            dt[t] = tile([P, S], F32, f"dt{t}", (None, None, "b_pos3", "b_neg3")[t])
             nc.vector.tensor_tensor(dt[t][:].indirect(l1[:]), pa[t][:], up[t][:], ALU.add)
 
         def put_smaller(t):
@@ -178,57 +187,36 @@ def tile_picked_kqorderwindwsum_none_po_kernel(tc, x_words, x_scales, w1_words, 
                 nc.scalar.activation(z_grouped[u][:, :, t], dt[t][:, u::PACK], ACT.Copy, scale=gains[:, t : t + 1])
 
         def second_projection(t):
-            project(b_ps[t], w2w, w2s, t, xb_w, xb_s)
+            project(b_ps[t][:], w2w, w2s, t, xb_w[:], xb_s[:])
             nc.scalar.copy(b_sb[t][:, :V], b_ps[t][:])
             nc.scalar.activation(b_pos[t][:], b_ps[t][:, :pe_cols], ACT.Copy, scale=gains[:, PACK + t : PACK + t + 1])
             nc.scalar.activation(b_neg[t][:], b_ps[t][:, :pe_cols], ACT.Copy, scale=gb_neg[:, t : t + 1])
-            nc.sync.dma_start(b_late[t][:], b_sb[t][:, :V])
-
-        last_term = []
 
         def fetch_term(t, sign):
-            term = tile([P, EARLY], F32, f"term{t}_{sign}")
+            term = tile([P, V], F32, f"term{t}_{sign}")
             lst, factor = ((l3, b_pos), (l4, b_neg))[sign]
-            nc.vector.tensor_tensor(term[:], b_sb[t][:].indirect(offsets(lst, 0, EARLY)), factor[t][:], ALU.mult)
-            last_term.append(term)
+            nc.vector.tensor_tensor(term[:], b_sb[t][:].indirect(lst[:]), factor[t][:], ALU.mult)
             return term
 
         def turn(t, plus, minus):
-            for j in range(EARLY // P):
-                cols = slice(P * j, P * (j + 1))
-                nc.tensor.matmul(turned[j][:, t, :], plus[:, cols], identity[:], is_transpose=True, start=True, stop=False)
-                nc.tensor.matmul(turned[j][:, t, :], minus[:, cols], identity[:], is_transpose=True, start=False, stop=True)
+            for term, opens in ((plus, True), (minus, False)):
+                for j in range(PACK):
+                    nc.tensor.matmul(turned[j][:, t, :], term[:, P * j : P * (j + 1)], identity[:], is_transpose=True, start=opens, stop=not opens)
 
-        def turn_back():
-            grouped = tile([P, EARLY, PACK], BF16, "z2_early")
-            pairs = [tile([P, 2, P, 2], BF16, f"pairs{j}") for j in range(EARLY // P)]
-            for j in range(EARLY // P):
-                nc.scalar.copy(pairs[j][:], turned[j][:].rearrange("v (w e) p -> v w p e", e=2))
-            for j in range(EARLY // P):
-                words = pairs[j][:].rearrange("v w p e -> v (w p e)").bitcast(F32)
-                back = psum.tile([P, 2, P], F32, name=f"back{j}", tag=f"bank{PACK + j}")
-                for w in range(2):
-                    nc.tensor.transpose(back[:, w, :], words[:, P * w : P * (w + 1)], identity[:])
-                nc.scalar.copy(
-                    grouped[:, P * j : P * (j + 1), :].rearrange("p v t -> p (v t)").bitcast(F32).rearrange("p (v w) -> p v w", w=2),
-                    back[:].rearrange("p w v -> p v w"),
-                )
-            return grouped
+        back = {}
 
-        late4, late_diff = {}, {}
-        z2_planes = tile([P, PACK, V - EARLY], BF16, "z2_planes")
+        def round_and_turn_back(j):
+            pairs = tile([P, 2, P, 2], BF16, f"pairs{j}")
+            nc.scalar.copy(pairs[:], turned[j][:].rearrange("v (w e) p -> v w p e", e=2))
+            words = pairs[:].rearrange("v w p e -> v (w p e)").bitcast(F32)
+            back[j] = psum.tile([P, 2, P], F32, name=f"back{j}", tag=f"bank{j}")
+            for w in range(2):
+                nc.tensor.transpose(back[j][:, w, :], words[:, P * w : P * (w + 1)], identity[:])
 
-        def fetch_late(t):
-            late4[t] = tile([P, V - EARLY], F32, f"late4_{t}", ("b_pos3", "b_neg3", "term3_0", "term3_1")[t])
-            nc.vector.tensor_copy(late4[t][:], b_late[t][:].indirect(offsets(l4, EARLY, V)))
-
-        def subtract_late(t):
-            late_diff[t] = tile([P, V - EARLY], F32, f"late_diff{t}", (None, "pairs1", "z2_early", "z_grouped0")[t])
-            nc.vector.tensor_tensor(late_diff[t][:], b_late[t][:].indirect(offsets(l3, EARLY, V)), late4[t][:], ALU.subtract)
-
-        def weigh_late(t):
-            nc.vector.scalar_tensor_tensor(
-                z2_planes[:, t, :], late_diff[t][:], gains[:, PACK + t : PACK + t + 1], b_late[t][:, EARLY:], ALU.mult, ALU.mult
+        def group_z2(j):
+            nc.scalar.copy(
+                z2_grouped[:, P * j : P * (j + 1), :].rearrange("p v t -> p (v t)").bitcast(F32).rearrange("p (v w) -> p v w", w=2),
+                back[j][:].rearrange("p w v -> p v w"),
             )
 
         fetch_first(0)
@@ -248,20 +236,21 @@ def tile_picked_kqorderwindwsum_none_po_kernel(tc, x_words, x_scales, w1_words, 
         fetch_difference(3)
         second_projection(2)
         second_projection(3)
-        turned = [psum.tile([P, PACK, P], F32, name=f"turned{j}", tag=f"bank{PACK + j}") for j in range(EARLY // P)]
-        put_larger(2)
-        plus = fetch_term(0, 0)
-        put_smaller(2)
-        turn(0, plus, fetch_term(0, 1))
-        for t in range(1, PACK):
-            turn(t, fetch_term(t, 0), fetch_term(t, 1))
-
-        z2_early = turn_back()
+        turned = [psum.tile([P, PACK, P], F32, name=f"turned{j}", tag=f"bank{j}") for j in range(PACK)]
         for t in range(PACK):
-            fetch_late(t)
-        subtract_late(0)
+            turn(t, fetch_term(t, 0), fetch_term(t, 1))
+        put_larger(2)
         put_larger(3)
-        subtract_late(1)
+        z2_grouped = tile([P, V, PACK], BF16, "z2_grouped")
+        for j in range(3):
+            round_and_turn_back(j)
+        negate(2)
+        round_and_turn_back(3)
+        group_z2(0)
+        negate(3)
+        for j in range(1, PACK):
+            group_z2(j)
+        put_smaller(2)
         put_smaller(3)
 
 
@@ -269,7 +258,7 @@ def tile_picked_kqorderwindwsum_none_po_kernel(tc, x_words, x_scales, w1_words, 
         z2_s = tile([P, V], U8, "z2_s")
         z_w = [tile([P, P], U32, f"z_w{u}") for u in range(PACK)]
         z_s = [tile([P, P], U8, f"z_s{u}") for u in range(PACK)]
-        s_ps = [psum.tile([P, V], F32, name=f"s_ps{u}", tag=f"bank{u}") for u in range(PACK)]
+        s_ps = [psum.tile([P, V], F32, name=f"s_ps{u}", tag=f"bank{PACK + u}") for u in range(PACK)]
         s_sb = [tile([P, 2 * V if u < 3 else V], F32, f"s_sb{u}") for u in range(PACK)]
         sig = [tile([P, V], F32, f"sig{u}") for u in range(PACK)]
 
@@ -279,9 +268,9 @@ def tile_picked_kqorderwindwsum_none_po_kernel(tc, x_words, x_scales, w1_words, 
         def own_sigmoid(u, lo, hi):
             nc.scalar.activation(sig[u][:, lo:hi], s_ps[u][:, lo:hi], ACT.Sigmoid, scale=0.0625)
 
-        def scores(u, lo, hi):
+        def scores(bank, u, lo, hi):
             nc.tensor.matmul_mx(
-                out=s_ps[u][:, lo:hi],
+                out=bank[:, lo:hi],
                 lhsT=z_w[u][:].bitcast(FP8X4),
                 lhsT_scale=z_s[u][:],
                 rhs=z2_w[:, lo:hi].bitcast(FP8X4),
@@ -290,34 +279,16 @@ def tile_picked_kqorderwindwsum_none_po_kernel(tc, x_words, x_scales, w1_words, 
                 stop=True,
             )
 
-        for lo, hi in ((0, HALF), (HALF, EARLY)):
-            quantize(z2_w[:, lo:hi], z2_s[:, lo:hi], z2_early[:, lo:hi, :])
-        def early_scores(u):
-            for lo, hi in ((0, HALF), (HALF, EARLY)):
-                scores(u, lo, hi)
-            leave_psum(u, 0, EARLY)
-            own_sigmoid(u, 0, EARLY)
-
-        subtract_late(2)
-        weigh_late(0)
-        weigh_late(1)
+        quantize(z2_w[:], z2_s[:], z2_grouped[:])
         quantize(z_w[0][:], z_s[0][:], z_grouped[0][:])
-        early_scores(0)
-        subtract_late(3)
-        quantize(z_w[1][:], z_s[1][:], z_grouped[1][:])
-        early_scores(1)
-        weigh_late(2)
-        weigh_late(3)
-        quantize(z_w[2][:], z_s[2][:], z_grouped[2][:])
-        z2_late = interleave(nc.vector.tensor_copy, z2_planes[:], "z2_late")
-        quantize(z_w[3][:], z_s[3][:], z_grouped[3][:])
-        quantize(z2_w[:, EARLY:], z2_s[:, EARLY:], z2_late[:])
-        scores(0, EARLY, V)
-        leave_psum(0, EARLY, V)
-        own_sigmoid(0, EARLY, V)
-        scores(1, EARLY, V)
-        for u in range(2, PACK):
-            scores(u, 0, V)
+        s_ps_high = psum.tile([P, V], F32, name="s_ps_high", tag="bank0")
+        for bank, lo, hi in ((s_ps[0], 0, HALF), (s_ps_high, HALF, V)):
+            scores(bank, 0, lo, hi)
+            nc.vector.tensor_scalar(s_sb[0][:, lo:hi], bank[:, lo:hi], 0.0625, None, ALU.mult)
+            nc.scalar.activation(sig[0][:, lo:hi], bank[:, lo:hi], ACT.Sigmoid, scale=0.0625)
+        for u in range(1, PACK):
+            quantize(z_w[u][:], z_s[u][:], z_grouped[u][:])
+            scores(s_ps[u], u, 0, V)
 
 
         y_w = tile([P, V], I32, "y_w")
@@ -325,21 +296,20 @@ def tile_picked_kqorderwindwsum_none_po_kernel(tc, x_words, x_scales, w1_words, 
         out_rows = out_0.rearrange("(p u) (g c) -> p u g c", u=PACK, c=QUARTER)
         out_words = out_1[0].rearrange("p c r -> p (c r)").bitcast(I32)
         y = tile([P, PACK, PACK, QUARTER], F32, "y")
-        units = [(0, 0, V), (1, 0, V), (2, 0, V), (3, 0, HALF), (3, HALF, HALF + QUARTER), (3, HALF + QUARTER, V)]
+        units = [(0, 0, V), (1, 0, V), (2, 0, V), (3, 0, HALF), (3, HALF, V)]
 
         def regroup(copy, lo, hi):
             grouped_y = tile([P, hi - lo, PACK], BF16, f"y_grouped{lo}")
-            for g in range(lo // QUARTER, hi // QUARTER):
-                copy(
-                    grouped_y[:, QUARTER * g - lo : QUARTER * (g + 1) - lo, :].rearrange("p (c i) u -> p c u i", i=4),
-                    y[:, g].rearrange("p u (c i) -> p c u i", i=4),
-                )
+            copy(
+                grouped_y[:].rearrange("p (g c i) u -> p g c u i", c=QUARTER // 4, i=4),
+                y[:, lo // QUARTER : hi // QUARTER].rearrange("p g u (c i) -> p g c u i", i=4),
+            )
             return grouped_y
 
         def add_turned():
             sums = {}
             for k in range(2):
-                sum_ps = psum.tile([P, PACK, P], F32, name=f"sum_ps{k}", tag=f"bank{PACK + k}")
+                sum_ps = psum.tile([P, PACK, P], F32, name=f"sum_ps{k}", tag=f"bank{1 + k}")
                 for g in range(PACK):
                     cols = slice(P * g, P * (g + 1))
                     nc.tensor.matmul(sum_ps[:, g, :], first[k][:, cols], identity[:], is_transpose=True, start=True, stop=False)
@@ -347,7 +317,7 @@ def tile_picked_kqorderwindwsum_none_po_kernel(tc, x_words, x_scales, w1_words, 
                 sums[k] = tile([P, PACK, P], F32, f"sums{k}")
                 nc.scalar.copy(sums[k][:], sum_ps[:])
             for k in range(2):
-                y_ps = psum.tile([P, PACK, P], F32, name=f"y_ps{k}", tag=f"bank{PACK + 2 + k}")
+                y_ps = psum.tile([P, PACK, P], F32, name=f"y_ps{k}", tag=f"bank{(3, 0)[k]}")
                 for g in range(PACK):
                     nc.tensor.transpose(y_ps[:, g, :], sums[k][:, g, :], identity[:])
                 nc.scalar.copy(y[:, :, k, :], y_ps[:])
@@ -355,11 +325,10 @@ def tile_picked_kqorderwindwsum_none_po_kernel(tc, x_words, x_scales, w1_words, 
 
         first = {}
         second = {}
-        y_grouped = {}
         for step in range(len(units) + 1):
             if step < len(units):
                 u, lo, hi = units[step]
-                done = EARLY if u == 1 else 0
+                done = 0
                 if u > 0 and lo == 0:
                     leave_psum(u, done, V)
                 if u > 0 and hi > done:
@@ -368,7 +337,8 @@ def tile_picked_kqorderwindwsum_none_po_kernel(tc, x_words, x_scales, w1_words, 
                 nc.scalar.activation(sig7[:], s_sb[u][:].indirect(offsets(l7, lo, hi)), ACT.Sigmoid)
                 first[step] = tile([P, hi - lo], F32, f"first{step}")
                 second[step] = tile([P, hi - lo], F32, f"second{step}")
-                nc.vector.tensor_tensor(first[step][:], s_sb[u][:].indirect(offsets(l5, lo, hi)), sig[u][:, lo:hi], ALU.mult)
+                for c0, c1 in ((0, HALF), (HALF, V)) if u == 0 else ((lo, hi),):
+                    nc.vector.tensor_tensor(first[step][:, c0 - lo : c1 - lo], s_sb[u][:].indirect(offsets(l5, c0, c1)), sig[u][:, c0:c1], ALU.mult)
             if 1 <= step:
                 pu, plo, phi = units[step - 1]
                 groups = slice(plo // QUARTER, phi // QUARTER)
@@ -379,20 +349,18 @@ def tile_picked_kqorderwindwsum_none_po_kernel(tc, x_words, x_scales, w1_words, 
                         second[step - 1][:].rearrange("p (g c) -> p g c", c=QUARTER),
                         ALU.add,
                     )
-                    if phi != HALF + QUARTER:
-                        stored = slice(0 if plo == 0 else 2, phi // QUARTER)
-                        nc.sync.dma_start(out_rows[:, pu, stored, :], y[:, stored, pu, :])
+                    nc.sync.dma_start(out_rows[:, pu, groups, :], y[:, groups, pu, :])
                 if step == len(units) - 1:
                     add_turned()
-                    y_grouped[0] = regroup(nc.scalar.copy, 0, HALF)
-                    y_grouped[1] = regroup(nc.scalar.copy, HALF, HALF + QUARTER)
+                    y_low = regroup(nc.scalar.copy, 0, HALF)
                 if step == len(units):
-                    y_grouped[2] = regroup(nc.vector.tensor_copy, HALF + QUARTER, V)
-                    quantize(y_w[:, :HALF], y_s[:, :HALF], y_grouped[0][:])
-                    quantize(y_w[:, HALF:EARLY], y_s[:, HALF:EARLY], y_grouped[1][:])
-                    nc.sync.dma_start(out_words[:, :EARLY], y_w[:, :EARLY])
-                    quantize(y_w[:, EARLY:], y_s[:, EARLY:], y_grouped[2][:])
-                    nc.scalar.dma_start(out_words[:, EARLY:], y_w[:, EARLY:])
+                    y_third = regroup(nc.scalar.copy, HALF, EARLY)
+                    y_last = regroup(nc.vector.tensor_copy, EARLY, V)
+                    quantize(y_w[:, :HALF], y_s[:, :HALF], y_low[:])
+                    nc.sync.dma_start(out_words[:, :HALF], y_w[:, :HALF])
+                    quantize(y_w[:, EARLY:], y_s[:, EARLY:], y_last[:])
+                    quantize(y_w[:, HALF:EARLY], y_s[:, HALF:EARLY], y_third[:])
+                    nc.scalar.dma_start(out_words[:, HALF:], y_w[:, HALF:])
             if step < len(units):
                 nc.vector.tensor_tensor(second[step][:], s_sb[u][:].indirect(offsets(l6, lo, hi)), sig7[:], ALU.mult)
         for q in range(4):

@@ -3,7 +3,7 @@ from contextlib import ExitStack
 import concourse.mybir as mybir
 from concourse.masks import make_identity
 
-K, T, S, V, H, W = 512, 2048, 512, 512, 512, 256
+T, S, V, H, W = 2048, 512, 512, 512, 256
 FLOPS = 3 * 2 * 512 * 512 * 512
 
 F32 = mybir.dt.float32
@@ -19,10 +19,13 @@ ACT = mybir.ActivationFunctionType
 
 P = 128
 PACK = 4
-HALF = 256
-QUARTER = 128
 BLOCKS = 16
-EARLY = 384
+HALF = 256
+LIST_COLUMN = 16
+LEAD = 512
+SCORE_SCALE = 0.0625
+TENSOR_SUMS = 1
+VECTOR_COPIES = 2
 
 
 def tile_picked_kqorderwindwsum_none_po_kernel(tc, x_words, x_scales, w1_words, w1_scales, w2_words, w2_scales, ga, gb, offs, two, n1, n2, n3, n4, n5, n6, n7, out_0, out_1, out_2):
@@ -31,17 +34,20 @@ def tile_picked_kqorderwindwsum_none_po_kernel(tc, x_words, x_scales, w1_words, 
         keep = ctx.enter_context(tc.tile_pool(name="keep", bufs=1))
         psum = ctx.enter_context(tc.psum_pool(name="psum", bufs=1))
 
-        def tile(shape, dtype, name, tag=None):
-            return keep.tile(shape, dtype, name=name, tag=tag or name, align_bytes=64)
+        def tile(shape, dtype, name, slot_of=None):
+            return keep.tile(shape, dtype, name=name, tag=slot_of or name, align_bytes=64)
+
+        def bank(shape, name, number):
+            return psum.tile(shape, F32, name=name, tag=f"bank{number}")
 
         def load_list(src, name):
             dst = tile(list(src.shape), U16, name)
             nc.sync.dma_start(dst[:], src)
             return dst
 
-        def zeroed_plane(width, name, engine):
-            plane = tile([P, width], U8, name)
-            engine.memset(plane[:].bitcast(I32), 0)
+        def zeroed_plane(name):
+            plane = tile([P, H], U8, name)
+            nc.vector.memset(plane[:].bitcast(I32), 0)
             return plane
 
         def load_scale_rows(plane, src, queues=(nc.sync, nc.sync)):
@@ -53,46 +59,49 @@ def tile_picked_kqorderwindwsum_none_po_kernel(tc, x_words, x_scales, w1_words, 
             nc.sync.dma_start(dst[:].bitcast(I32), src[0].bitcast(I32))
             return dst
 
-        def deal(raw, name, tag=None):
-            dst = tile(list(raw.shape), U8, name, tag)
+        def deal(raw, name, slot_of=None):
+            dst = tile(list(raw.shape), U8, name, slot_of)
             nc.vector.tensor_copy(
-                dst[:].bitcast(I32).rearrange("p (t b e) -> p b t e", t=PACK, b=BLOCKS),
-                raw[:].bitcast(I32).rearrange("p (b t e) -> p b t e", t=PACK, b=BLOCKS),
+                dst[:].bitcast(I32).rearrange("p (t c e) -> p c t e", t=PACK, c=BLOCKS),
+                raw[:].bitcast(I32).rearrange("p (c t e) -> p c t e", t=PACK, c=BLOCKS),
             )
             return dst
 
-        def interleave(copy, planes, name):
-            width = planes.shape[2]
-            grouped = tile([P, width, PACK], BF16, name)
-            copy(grouped[:].rearrange("p (c i) t -> p c t i", i=4), planes.rearrange("p t (c i) -> p c t i", i=4))
-            return grouped
+        def multiply(out, lhs_words, lhs_scales, rhs_words, rhs_scales):
+            nc.tensor.matmul_mx(out=out, lhsT=lhs_words, lhsT_scale=lhs_scales, rhs=rhs_words, rhs_scale=rhs_scales, start=True, stop=True)
+
+        def project(out, words, scales, t, x_w, x_s):
+            multiply(out, words[:, 2 * P * t : 2 * P * (t + 1)].bitcast(FP4X4), scales[:, P * t : P * (t + 1)], x_w.bitcast(FP8X4), x_s)
 
         def quantize(words, scales, grouped):
-            nc.vector.quantize_mx(out=words.bitcast(FP8X4), scales=scales, in_=grouped.rearrange("p c t -> p (c t)"))
+            nc.vector.quantize_mx(out=words.bitcast(FP8X4), scales=scales, in_=grouped[:].rearrange("p c t -> p (c t)"))
 
-        def offsets(lst, lo, hi):
-            return lst[:, lo // 16 : hi // 16]
+        def turn(out, src, opens, closes):
+            nc.tensor.matmul(out, src, identity[:], is_transpose=True, start=opens, stop=closes)
 
-        xs = tile([P, T], U8, "xs")
-        nc.gpsimd.memset(xs[:, : T // 2].bitcast(I32), 0)
-        nc.vector.memset(xs[:, T // 2 :].bitcast(I32), 0)
-        w1s_raw = zeroed_plane(H, "w1s_raw", nc.vector)
-        w2s_raw = zeroed_plane(H, "w2s_raw", nc.vector)
+        def entries(lst, lo, hi):
+            return lst[:, lo // LIST_COLUMN : hi // LIST_COLUMN]
+
+        x_scale_table = tile([P, T], U8, "x_scale_table")
+        nc.gpsimd.memset(x_scale_table[:, : T // 2].bitcast(I32), 0)
+        nc.vector.memset(x_scale_table[:, T // 2 :].bitcast(I32), 0)
+        w1s_raw = zeroed_plane("w1s_raw")
+        w2s_raw = zeroed_plane("w2s_raw")
         gain_rows = tile([P, P], F32, "gain_rows")
         nc.vector.memset(gain_rows[:], 0.0)
-
         identity = tile([P, P], F32, "identity")
         make_identity(nc, identity[:])
+
         warm_out = tile([P, 1], F32, "warm_out")
         nc.scalar.activation(warm_out[:], identity[:, 0:1], ACT.Sigmoid)
 
-        xw = tile([P, T], I32, "xw")
+        x_word_table = tile([P, T], I32, "x_word_table")
         x_view = x_words[0].rearrange("p c r -> p (c r)").bitcast(I32)
-        nc.sync.dma_start(xw[:, :512], x_view[:, :512])
+        nc.sync.dma_start(x_word_table[:, :LEAD], x_view[:, :LEAD])
         l_offs = load_list(offs, "l_offs")
-        load_scale_rows(xs, x_scales, (nc.sync, nc.scalar))
+        load_scale_rows(x_scale_table, x_scales, (nc.sync, nc.scalar))
         l_two = load_list(two, "l_two")
-        nc.sync.dma_start(xw[:, 512:], x_view[:, 512:])
+        nc.sync.dma_start(x_word_table[:, LEAD:], x_view[:, LEAD:])
         w1w_raw = load_weight_words(w1_words, "w1w_raw")
         load_scale_rows(w1s_raw, w1_scales)
         l1 = load_list(n1, "l1")
@@ -101,8 +110,8 @@ def tile_picked_kqorderwindwsum_none_po_kernel(tc, x_words, x_scales, w1_words, 
         load_scale_rows(w2s_raw, w2_scales)
         for j, gain in enumerate((ga, gb)):
             nc.sync.dma_start(
-                gain_rows[PACK * j : PACK * (j + 1), :].rearrange("t (b r) -> t b r", b=BLOCKS),
-                gain.rearrange("(b t r) o -> t b (r o)", b=BLOCKS, t=PACK),
+                gain_rows[PACK * j : PACK * (j + 1), :].rearrange("t (c r) -> t c r", c=BLOCKS),
+                gain.rearrange("(c t r) o -> t c (r o)", c=BLOCKS, t=PACK),
             )
         l4 = load_list(n4, "l4")
         l3 = load_list(n3, "l3")
@@ -113,95 +122,83 @@ def tile_picked_kqorderwindwsum_none_po_kernel(tc, x_words, x_scales, w1_words, 
         xb_s = tile([P, V], U8, "xb_s")
         xa_s = tile([P, S], U8, "xa_s")
         xa_w = tile([P, S], U32, "xa_w")
-        nc.vector.tensor_copy(xa_s[:], xs[:].indirect(l_offs[:]))
-        nc.vector.tensor_copy(xb_s[:], xs[:].indirect(l_two[:]))
-        nc.vector.tensor_copy(xa_w[:], xw[:].bitcast(U32).indirect(l_offs[:]))
+        nc.vector.tensor_copy(xa_s[:], x_scale_table[:].indirect(l_offs[:]))
+        nc.vector.tensor_copy(xb_s[:], x_scale_table[:].indirect(l_two[:]))
+        nc.vector.tensor_copy(xa_w[:], x_word_table[:].bitcast(U32).indirect(l_offs[:]))
         w1w = deal(w1w_raw, "w1w")
         w1s = deal(w1s_raw, "w1s")
-        xb_w = tile([P, V], U32, "xb_w", tag="w1s_raw")
-        nc.vector.tensor_copy(xb_w[:], xw[:].bitcast(U32).indirect(l_two[:]))
+        xb_w = tile([P, V], U32, "xb_w", "w1s_raw")
+        nc.vector.tensor_copy(xb_w[:], x_word_table[:].bitcast(U32).indirect(l_two[:]))
         w2w = deal(w2w_raw, "w2w")
 
-        def project(bank, ww, ws, t, xw_g, xs_g):
-            nc.tensor.matmul_mx(
-                out=bank,
-                lhsT=ww[:, 2 * P * t : 2 * P * (t + 1)].bitcast(FP4X4),
-                lhsT_scale=ws[:, P * t : P * (t + 1)],
-                rhs=xw_g.bitcast(FP8X4),
-                rhs_scale=xs_g,
-                start=True,
-                stop=True,
-            )
-
-        a_ps = [psum.tile([P, S], F32, name=f"a_ps{t}", tag=f"bank{t}") for t in range(PACK)]
+        a_ps = [bank([P, S], f"a_ps{t}", t) for t in range(PACK)]
         a_sb = [tile([P, S], F32, f"a_sb{t}") for t in range(PACK)]
-        a_ps_high = psum.tile([P, S], F32, name="a_ps_high", tag="bank7")
-        for bank, cols in ((a_ps[0], slice(0, HALF)), (a_ps_high, slice(HALF, S))):
-            project(bank[:, cols], w1w, w1s, 0, xa_w[:, cols], xa_s[:, cols])
-            nc.scalar.copy(a_sb[0][:, cols], bank[:, cols])
+        a_ps_high = bank([P, S], "a_ps_high", 7)
+        for half_ps, cols in ((a_ps[0], slice(0, HALF)), (a_ps_high, slice(HALF, S))):
+            project(half_ps[:, cols], w1w, w1s, 0, xa_w[:, cols], xa_s[:, cols])
+            nc.scalar.copy(a_sb[0][:, cols], half_ps[:, cols])
         for t in range(1, PACK):
             project(a_ps[t][:], w1w, w1s, t, xa_w[:], xa_s[:])
             nc.scalar.copy(a_sb[t][:], a_ps[t][:])
 
-        gains_ps = psum.tile([P, V], F32, name="gains_ps", tag="bank0")
+        gains_ps = bank([P, P], "gains_ps", 0)
         gains = tile([P, 2 * PACK], F32, "gains")
-        nc.tensor.transpose(gains_ps[:, :P], gain_rows[:], identity[:])
+        nc.tensor.transpose(gains_ps[:], gain_rows[:], identity[:])
         nc.scalar.copy(gains[:], gains_ps[:, : 2 * PACK])
         gb_neg = tile([P, PACK], F32, "gb_neg")
         nc.scalar.activation(gb_neg[:], gains_ps[:, PACK : 2 * PACK], ACT.Copy, scale=-1.0)
 
-        b_ps = [psum.tile([P, V], F32, name=f"b_ps{t}", tag=f"bank{PACK + t}") for t in range(PACK)]
-        b_sb = [tile([P, 2 * V], F32, f"b_sb{t}") for t in range(PACK)]
-        pe_cols = V
-        b_pos = [tile([P, pe_cols], F32, f"b_pos{t}") for t in range(PACK)]
-        b_neg = [tile([P, pe_cols], F32, f"b_neg{t}") for t in range(PACK)]
-
         z_grouped = [tile([P, P, PACK], BF16, f"z_grouped{u}") for u in range(PACK)]
-        pa, diff, up, down_abs, down, dt = {}, {}, {}, {}, {}, {}
+        pa, diff, up, down_size, down, dt = {}, {}, {}, {}, {}, {}
 
-        def fetch_first(t):
-            pa[t] = tile([P, W], F32, f"pa{t}", (None, None, "diff0", "diff1")[t])
+        def fetch_first(t, slot_of=None):
+            pa[t] = tile([P, W], F32, f"pa{t}", slot_of)
             nc.vector.tensor_copy(pa[t][:], a_sb[t][:].indirect(l1[:]))
 
-        def fetch_difference(t):
-            diff[t] = tile([P, W], F32, f"diff{t}", (None, None, "up0", "up1")[t])
+        def fetch_difference(t, slot_of=None):
+            diff[t] = tile([P, W], F32, f"diff{t}", slot_of)
             nc.vector.tensor_tensor(diff[t][:], a_sb[t][:].indirect(l2[:]), pa[t][:], ALU.subtract)
-            down_abs[t] = tile([P, W], F32, f"down_abs{t}")
+            down_size[t] = tile([P, W], F32, f"down_size{t}")
+            nc.scalar.activation(down_size[t][:], diff[t][:], ACT.Relu, scale=-1.0)
+
+        def step_down(t, slot_of=None):
+            down[t] = tile([P, W], F32, f"down{t}", slot_of)
+            nc.scalar.activation(down[t][:], down_size[t][:], ACT.Copy, scale=-1.0)
+
+        def step_up(t):
             up[t] = tile([P, W], F32, f"up{t}")
-            nc.scalar.activation(down_abs[t][:], diff[t][:], ACT.Relu, scale=-1.0)
-            if t < 2:
-                negate(t)
             nc.scalar.activation(up[t][:], diff[t][:], ACT.Relu)
 
-        def negate(t):
-            down[t] = tile([P, W], F32, f"down{t}", (None, None, "pairs0", "pairs2")[t])
-            nc.scalar.activation(down[t][:], down_abs[t][:], ACT.Copy, scale=-1.0)
-
-        def put_larger(t):
-            dt[t] = tile([P, S], F32, f"dt{t}", (None, None, "b_pos3", "b_neg3")[t])
+        def put_larger(t, slot_of=None):
+            dt[t] = tile([P, S], F32, f"dt{t}", slot_of)
             nc.vector.tensor_tensor(dt[t][:].indirect(l1[:]), pa[t][:], up[t][:], ALU.add)
 
         def put_smaller(t):
             nc.vector.tensor_tensor(dt[t][:].indirect(l2[:]), pa[t][:], down[t][:], ALU.add)
+
+        def round_z(t):
             for u in range(PACK):
                 nc.scalar.activation(z_grouped[u][:, :, t], dt[t][:, u::PACK], ACT.Copy, scale=gains[:, t : t + 1])
+
+        b_ps = [bank([P, V], f"b_ps{t}", PACK + t) for t in range(PACK)]
+        b_sb = [tile([P, 2 * V], F32, f"b_sb{t}") for t in range(PACK)]
+        b_pos = [tile([P, V], F32, f"b_pos{t}") for t in range(PACK)]
+        b_neg = [tile([P, V], F32, f"b_neg{t}") for t in range(PACK)]
 
         def second_projection(t):
             project(b_ps[t][:], w2w, w2s, t, xb_w[:], xb_s[:])
             nc.scalar.copy(b_sb[t][:, :V], b_ps[t][:])
-            nc.scalar.activation(b_pos[t][:], b_ps[t][:, :pe_cols], ACT.Copy, scale=gains[:, PACK + t : PACK + t + 1])
-            nc.scalar.activation(b_neg[t][:], b_ps[t][:, :pe_cols], ACT.Copy, scale=gb_neg[:, t : t + 1])
+            nc.scalar.activation(b_pos[t][:], b_ps[t][:], ACT.Copy, scale=gains[:, PACK + t : PACK + t + 1])
+            nc.scalar.activation(b_neg[t][:], b_ps[t][:], ACT.Copy, scale=gb_neg[:, t : t + 1])
 
-        def fetch_term(t, sign):
-            term = tile([P, V], F32, f"term{t}_{sign}")
-            lst, factor = ((l3, b_pos), (l4, b_neg))[sign]
-            nc.vector.tensor_tensor(term[:], b_sb[t][:].indirect(lst[:]), factor[t][:], ALU.mult)
-            return term
-
-        def turn(t, plus, minus):
+        def add_terms(t):
+            plus = tile([P, V], F32, f"plus{t}")
+            minus = tile([P, V], F32, f"minus{t}")
+            nc.vector.tensor_tensor(plus[:], b_sb[t][:].indirect(l3[:]), b_pos[t][:], ALU.mult)
+            nc.vector.tensor_tensor(minus[:], b_sb[t][:].indirect(l4[:]), b_neg[t][:], ALU.mult)
             for term, opens in ((plus, True), (minus, False)):
                 for j in range(PACK):
-                    nc.tensor.matmul(turned[j][:, t, :], term[:, P * j : P * (j + 1)], identity[:], is_transpose=True, start=opens, stop=not opens)
+                    turn(turned[j][:, t, :], term[:, P * j : P * (j + 1)], opens, not opens)
 
         back = {}
 
@@ -209,7 +206,7 @@ def tile_picked_kqorderwindwsum_none_po_kernel(tc, x_words, x_scales, w1_words, 
             pairs = tile([P, 2, P, 2], BF16, f"pairs{j}")
             nc.scalar.copy(pairs[:], turned[j][:].rearrange("v (w e) p -> v w p e", e=2))
             words = pairs[:].rearrange("v w p e -> v (w p e)").bitcast(F32)
-            back[j] = psum.tile([P, 2, P], F32, name=f"back{j}", tag=f"bank{j}")
+            back[j] = bank([P, 2, P], f"back{j}", j)
             for w in range(2):
                 nc.tensor.transpose(back[j][:, w, :], words[:, P * w : P * (w + 1)], identity[:])
 
@@ -219,150 +216,151 @@ def tile_picked_kqorderwindwsum_none_po_kernel(tc, x_words, x_scales, w1_words, 
                 back[j][:].rearrange("p w v -> p v w"),
             )
 
-        fetch_first(0)
-        fetch_difference(0)
-        fetch_first(1)
-        w2s = deal(w2s_raw, "w2s", "a_sb0")
-        fetch_difference(1)
+        for t in range(2):
+            fetch_first(t)
+            if t == 1:
+                w2s = deal(w2s_raw, "w2s", "a_sb0")
+            fetch_difference(t)
+            step_down(t)
+            step_up(t)
         put_larger(0)
-        fetch_first(2)
+        fetch_first(2, "diff0")
         put_smaller(0)
-        fetch_difference(2)
+        round_z(0)
+        fetch_difference(2, "up0")
+        step_up(2)
         second_projection(0)
         second_projection(1)
-        put_larger(1)
-        fetch_first(3)
+        put_larger(1, "w2w")
+        fetch_first(3, "diff1")
         put_smaller(1)
-        fetch_difference(3)
+        fetch_difference(3, "up1")
+        step_up(3)
         second_projection(2)
         second_projection(3)
-        turned = [psum.tile([P, PACK, P], F32, name=f"turned{j}", tag=f"bank{j}") for j in range(PACK)]
+        round_z(1)
+
+        turned = [bank([P, PACK, P], f"turned{j}", j) for j in range(PACK)]
         for t in range(PACK):
-            turn(t, fetch_term(t, 0), fetch_term(t, 1))
-        put_larger(2)
-        put_larger(3)
+            add_terms(t)
+        put_larger(2, "b_pos3")
+        put_larger(3, "b_neg3")
         z2_grouped = tile([P, V, PACK], BF16, "z2_grouped")
-        for j in range(3):
+        for j in range(PACK - 1):
             round_and_turn_back(j)
-        negate(2)
-        round_and_turn_back(3)
+        step_down(2, "pairs0")
+        round_and_turn_back(PACK - 1)
         group_z2(0)
-        negate(3)
+        step_down(3, "pairs2")
         for j in range(1, PACK):
             group_z2(j)
-        put_smaller(2)
-        put_smaller(3)
-
+        for t in range(2, PACK):
+            put_smaller(t)
+            round_z(t)
 
         z2_w = tile([P, V], U32, "z2_w")
         z2_s = tile([P, V], U8, "z2_s")
         z_w = [tile([P, P], U32, f"z_w{u}") for u in range(PACK)]
         z_s = [tile([P, P], U8, f"z_s{u}") for u in range(PACK)]
-        s_ps = [psum.tile([P, V], F32, name=f"s_ps{u}", tag=f"bank{PACK + u}") for u in range(PACK)]
-        s_sb = [tile([P, 2 * V if u < 3 else V], F32, f"s_sb{u}") for u in range(PACK)]
+        s_ps = [bank([P, V], f"s_ps{u}", PACK + u) for u in range(PACK)]
+        s_sb = [tile([P, 2 * V if u < PACK - 1 else V], F32, f"s_sb{u}") for u in range(PACK)]
         sig = [tile([P, V], F32, f"sig{u}") for u in range(PACK)]
 
-        def leave_psum(u, lo, hi):
-            nc.scalar.activation(s_sb[u][:, lo:hi], s_ps[u][:, lo:hi], ACT.Copy, scale=0.0625)
+        def scores(out, u, cols):
+            multiply(out[:, cols], z_w[u][:].bitcast(FP8X4), z_s[u][:], z2_w[:, cols].bitcast(FP8X4), z2_s[:, cols])
 
-        def own_sigmoid(u, lo, hi):
-            nc.scalar.activation(sig[u][:, lo:hi], s_ps[u][:, lo:hi], ACT.Sigmoid, scale=0.0625)
-
-        def scores(bank, u, lo, hi):
-            nc.tensor.matmul_mx(
-                out=bank[:, lo:hi],
-                lhsT=z_w[u][:].bitcast(FP8X4),
-                lhsT_scale=z_s[u][:],
-                rhs=z2_w[:, lo:hi].bitcast(FP8X4),
-                rhs_scale=z2_s[:, lo:hi],
-                start=True,
-                stop=True,
-            )
-
-        quantize(z2_w[:], z2_s[:], z2_grouped[:])
-        quantize(z_w[0][:], z_s[0][:], z_grouped[0][:])
-        s_ps_high = psum.tile([P, V], F32, name="s_ps_high", tag="bank0")
-        for bank, lo, hi in ((s_ps[0], 0, HALF), (s_ps_high, HALF, V)):
-            scores(bank, 0, lo, hi)
-            nc.vector.tensor_scalar(s_sb[0][:, lo:hi], bank[:, lo:hi], 0.0625, None, ALU.mult)
-            nc.scalar.activation(sig[0][:, lo:hi], bank[:, lo:hi], ACT.Sigmoid, scale=0.0625)
+        quantize(z2_w[:], z2_s[:], z2_grouped)
+        quantize(z_w[0][:], z_s[0][:], z_grouped[0])
+        s_ps_high = bank([P, V], "s_ps_high", 0)
+        for half_ps, cols in ((s_ps[0], slice(0, HALF)), (s_ps_high, slice(HALF, V))):
+            scores(half_ps, 0, cols)
+            nc.vector.tensor_scalar(s_sb[0][:, cols], half_ps[:, cols], SCORE_SCALE, None, ALU.mult)
+            nc.scalar.activation(sig[0][:, cols], half_ps[:, cols], ACT.Sigmoid, scale=SCORE_SCALE)
         for u in range(1, PACK):
-            quantize(z_w[u][:], z_s[u][:], z_grouped[u][:])
-            scores(s_ps[u], u, 0, V)
-
+            quantize(z_w[u][:], z_s[u][:], z_grouped[u])
+            scores(s_ps[u], u, slice(0, V))
 
         y_w = tile([P, V], I32, "y_w")
         y_s = tile([P, V], U8, "y_s")
-        out_rows = out_0.rearrange("(p u) (g c) -> p u g c", u=PACK, c=QUARTER)
+        out_rows = out_0.rearrange("(p u) (g c) -> p u g c", u=PACK, c=P)
         out_words = out_1[0].rearrange("p c r -> p (c r)").bitcast(I32)
-        y = tile([P, PACK, PACK, QUARTER], F32, "y")
-        units = [(0, 0, V), (1, 0, V), (2, 0, V), (3, 0, HALF), (3, HALF, V)]
+        y = tile([P, PACK, PACK, P], F32, "y")
+        pieces = [(u, 0, V) for u in range(PACK - 1)] + [(PACK - 1, 0, HALF), (PACK - 1, HALF, V)]
+        first, second, sig7 = {}, {}, {}
+
+        def first_term(k):
+            u, lo, hi = pieces[k]
+            if u > 0:
+                if u < VECTOR_COPIES:
+                    nc.vector.tensor_scalar(s_sb[u][:, :V], s_ps[u][:], SCORE_SCALE, None, ALU.mult)
+                elif lo == 0:
+                    nc.scalar.activation(s_sb[u][:, :V], s_ps[u][:], ACT.Copy, scale=SCORE_SCALE)
+                nc.scalar.activation(sig[u][:, lo:hi], s_ps[u][:, lo:hi], ACT.Sigmoid, scale=SCORE_SCALE)
+            sig7[k] = tile([P, hi - lo], F32, f"sig7_{k}")
+            nc.scalar.activation(sig7[k][:], s_sb[u][:].indirect(entries(l7, lo, hi)), ACT.Sigmoid)
+            first[k] = tile([P, hi - lo], F32, f"first{k}")
+            for c0, c1 in ((0, HALF), (HALF, V)) if u == 0 else ((lo, hi),):
+                nc.vector.tensor_tensor(first[k][:, c0 - lo : c1 - lo], s_sb[u][:].indirect(entries(l5, c0, c1)), sig[u][:, c0:c1], ALU.mult)
+
+        def second_term(k):
+            u, lo, hi = pieces[k]
+            second[k] = tile([P, hi - lo], F32, f"second{k}")
+            nc.vector.tensor_tensor(second[k][:], s_sb[u][:].indirect(entries(l6, lo, hi)), sig7[k][:], ALU.mult)
+
+        def add_on_vector(k):
+            u, lo, hi = pieces[k]
+            groups = slice(lo // P, hi // P)
+            nc.vector.tensor_tensor(
+                y[:, groups, u, :],
+                first[k][:].rearrange("p (g c) -> p g c", c=P),
+                second[k][:].rearrange("p (g c) -> p g c", c=P),
+                ALU.add,
+            )
+            nc.sync.dma_start(out_rows[:, u, groups, :], y[:, groups, u, :])
+
+        def add_on_tensor():
+            sums = {}
+            for u in range(TENSOR_SUMS):
+                sum_ps = bank([P, PACK, P], f"sum_ps{u}", 1 + u)
+                for g in range(PACK):
+                    turn(sum_ps[:, g, :], first[u][:, P * g : P * (g + 1)], True, False)
+                    turn(sum_ps[:, g, :], second[u][:, P * g : P * (g + 1)], False, True)
+                sums[u] = tile([P, PACK, P], F32, f"sums{u}")
+                nc.scalar.copy(sums[u][:], sum_ps[:])
+            for u in range(TENSOR_SUMS):
+                y_ps = bank([P, PACK, P], f"y_ps{u}", (3 + u) % PACK)
+                for g in range(PACK):
+                    nc.tensor.transpose(y_ps[:, g, :], sums[u][:, g, :], identity[:])
+                nc.scalar.copy(y[:, :, u, :], y_ps[:])
+                nc.sync.dma_start(out_rows[:, u, :, :], y[:, :, u, :])
 
         def regroup(copy, lo, hi):
-            grouped_y = tile([P, hi - lo, PACK], BF16, f"y_grouped{lo}")
+            grouped = tile([P, hi - lo, PACK], BF16, f"y_grouped{lo}")
             copy(
-                grouped_y[:].rearrange("p (g c i) u -> p g c u i", c=QUARTER // 4, i=4),
-                y[:, lo // QUARTER : hi // QUARTER].rearrange("p g u (c i) -> p g c u i", i=4),
+                grouped[:].rearrange("p (g c i) u -> p g c u i", c=P // 4, i=4),
+                y[:, lo // P : hi // P].rearrange("p g u (c i) -> p g c u i", i=4),
             )
-            return grouped_y
+            return grouped
 
-        def add_turned():
-            sums = {}
-            for k in range(2):
-                sum_ps = psum.tile([P, PACK, P], F32, name=f"sum_ps{k}", tag=f"bank{1 + k}")
-                for g in range(PACK):
-                    cols = slice(P * g, P * (g + 1))
-                    nc.tensor.matmul(sum_ps[:, g, :], first[k][:, cols], identity[:], is_transpose=True, start=True, stop=False)
-                    nc.tensor.matmul(sum_ps[:, g, :], second[k][:, cols], identity[:], is_transpose=True, start=False, stop=True)
-                sums[k] = tile([P, PACK, P], F32, f"sums{k}")
-                nc.scalar.copy(sums[k][:], sum_ps[:])
-            for k in range(2):
-                y_ps = psum.tile([P, PACK, P], F32, name=f"y_ps{k}", tag=f"bank{(3, 0)[k]}")
-                for g in range(PACK):
-                    nc.tensor.transpose(y_ps[:, g, :], sums[k][:, g, :], identity[:])
-                nc.scalar.copy(y[:, :, k, :], y_ps[:])
-                nc.sync.dma_start(out_rows[:, k, :, :], y[:, :, k, :])
+        last = len(pieces) - 1
+        for k in range(len(pieces)):
+            first_term(k)
+            if k > TENSOR_SUMS:
+                add_on_vector(k - 1)
+            if k == last:
+                add_on_tensor()
+                y_low = regroup(nc.scalar.copy, 0, HALF)
+            second_term(k)
+        add_on_vector(last)
 
-        first = {}
-        second = {}
-        for step in range(len(units) + 1):
-            if step < len(units):
-                u, lo, hi = units[step]
-                done = 0
-                if u > 0 and lo == 0:
-                    leave_psum(u, done, V)
-                if u > 0 and hi > done:
-                    own_sigmoid(u, max(lo, done), hi)
-                sig7 = tile([P, hi - lo], F32, f"sig7_{step}")
-                nc.scalar.activation(sig7[:], s_sb[u][:].indirect(offsets(l7, lo, hi)), ACT.Sigmoid)
-                first[step] = tile([P, hi - lo], F32, f"first{step}")
-                second[step] = tile([P, hi - lo], F32, f"second{step}")
-                for c0, c1 in ((0, HALF), (HALF, V)) if u == 0 else ((lo, hi),):
-                    nc.vector.tensor_tensor(first[step][:, c0 - lo : c1 - lo], s_sb[u][:].indirect(offsets(l5, c0, c1)), sig[u][:, c0:c1], ALU.mult)
-            if 1 <= step:
-                pu, plo, phi = units[step - 1]
-                groups = slice(plo // QUARTER, phi // QUARTER)
-                if pu >= 2:
-                    nc.vector.tensor_tensor(
-                        y[:, groups, pu, :],
-                        first[step - 1][:].rearrange("p (g c) -> p g c", c=QUARTER),
-                        second[step - 1][:].rearrange("p (g c) -> p g c", c=QUARTER),
-                        ALU.add,
-                    )
-                    nc.sync.dma_start(out_rows[:, pu, groups, :], y[:, groups, pu, :])
-                if step == len(units) - 1:
-                    add_turned()
-                    y_low = regroup(nc.scalar.copy, 0, HALF)
-                if step == len(units):
-                    y_third = regroup(nc.scalar.copy, HALF, EARLY)
-                    y_last = regroup(nc.vector.tensor_copy, EARLY, V)
-                    quantize(y_w[:, :HALF], y_s[:, :HALF], y_low[:])
-                    nc.sync.dma_start(out_words[:, :HALF], y_w[:, :HALF])
-                    quantize(y_w[:, EARLY:], y_s[:, EARLY:], y_last[:])
-                    quantize(y_w[:, HALF:EARLY], y_s[:, HALF:EARLY], y_third[:])
-                    nc.scalar.dma_start(out_words[:, HALF:], y_w[:, HALF:])
-            if step < len(units):
-                nc.vector.tensor_tensor(second[step][:], s_sb[u][:].indirect(offsets(l6, lo, hi)), sig7[:], ALU.mult)
+        third = HALF + P
+        y_third = regroup(nc.scalar.copy, HALF, third)
+        y_last = regroup(nc.vector.tensor_copy, third, V)
+        quantize(y_w[:, :HALF], y_s[:, :HALF], y_low)
+        nc.sync.dma_start(out_words[:, :HALF], y_w[:, :HALF])
+        quantize(y_w[:, third:], y_s[:, third:], y_last)
+        quantize(y_w[:, HALF:third], y_s[:, HALF:third], y_third)
+        nc.scalar.dma_start(out_words[:, HALF:], y_w[:, HALF:])
         for q in range(4):
             queue = nc.scalar if q % 2 else nc.sync
             queue.dma_start(out_2[0, 4 * q : 4 * q + 4, :].bitcast(I32), y_s[32 * q : 32 * q + 4, :].bitcast(I32))

@@ -92,9 +92,6 @@ def tile_picked_kqorderwindwsum_none_po_kernel(tc, x_words, x_scales, w1_words, 
         identity = tile([P, P], F32, "identity")
         make_identity(nc, identity[:])
 
-        warm_out = tile([P, 1], F32, "warm_out")
-        nc.scalar.activation(warm_out[:], identity[:, 0:1], ACT.Sigmoid)
-
         x_word_table = tile([P, T], I32, "x_word_table")
         x_view = x_words[0].rearrange("p c r -> p (c r)").bitcast(I32)
         nc.sync.dma_start(x_word_table[:, :LEAD], x_view[:, :LEAD])

from contextlib import ExitStack

import concourse.mybir as mybir
from concourse.masks import make_identity

T, S, V, H, W = 2048, 512, 512, 512, 256
FLOPS = 3 * 2 * 512 * 512 * 512

F32 = mybir.dt.float32
BF16 = mybir.dt.bfloat16
I32 = mybir.dt.int32
U32 = mybir.dt.uint32
U16 = mybir.dt.uint16
U8 = mybir.dt.uint8
FP8X4 = mybir.dt.float8_e4m3fn_x4
FP4X4 = mybir.dt.float4_e2m1fn_x4
ALU = mybir.AluOpType
ACT = mybir.ActivationFunctionType

P = 128
PACK = 4
BLOCKS = 16
HALF = 256
LIST_COLUMN = 16
LEAD = 512
SCORE_SCALE = 0.0625
TENSOR_SUMS = 1
VECTOR_COPIES = 2


def tile_picked_kqorderwindwsum_none_po_kernel(tc, x_words, x_scales, w1_words, w1_scales, w2_words, w2_scales, ga, gb, offs, two, n1, n2, n3, n4, n5, n6, n7, out_0, out_1, out_2):
    nc = tc.nc
    with ExitStack() as ctx:
        keep = ctx.enter_context(tc.tile_pool(name="keep", bufs=1))
        psum = ctx.enter_context(tc.psum_pool(name="psum", bufs=1))

        def tile(shape, dtype, name, slot_of=None):
            return keep.tile(shape, dtype, name=name, tag=slot_of or name, align_bytes=64)

        def bank(shape, name, number):
            return psum.tile(shape, F32, name=name, tag=f"bank{number}")

        def load_list(src, name):
            dst = tile(list(src.shape), U16, name)
            nc.sync.dma_start(dst[:], src)
            return dst

        def zeroed_plane(name):
            plane = tile([P, H], U8, name)
            nc.vector.memset(plane[:].bitcast(I32), 0)
            return plane

        def load_scale_rows(plane, src, queues=(nc.sync, nc.sync)):
            for q in range(4):
                queues[q % 2].dma_start(plane[32 * q : 32 * q + 4, :].bitcast(I32), src[0, 4 * q : 4 * q + 4, :].bitcast(I32))

        def load_weight_words(src, name):
            dst = tile([P, 2 * H], U8, name)
            nc.sync.dma_start(dst[:].bitcast(I32), src[0].bitcast(I32))
            return dst

        def deal(raw, name, slot_of=None):
            dst = tile(list(raw.shape), U8, name, slot_of)
            nc.vector.tensor_copy(
                dst[:].bitcast(I32).rearrange("p (t c e) -> p c t e", t=PACK, c=BLOCKS),
                raw[:].bitcast(I32).rearrange("p (c t e) -> p c t e", t=PACK, c=BLOCKS),
            )
            return dst

        def multiply(out, lhs_words, lhs_scales, rhs_words, rhs_scales):
            nc.tensor.matmul_mx(out=out, lhsT=lhs_words, lhsT_scale=lhs_scales, rhs=rhs_words, rhs_scale=rhs_scales, start=True, stop=True)

        def project(out, words, scales, t, x_w, x_s):
            multiply(out, words[:, 2 * P * t : 2 * P * (t + 1)].bitcast(FP4X4), scales[:, P * t : P * (t + 1)], x_w.bitcast(FP8X4), x_s)

        def quantize(words, scales, grouped):
            nc.vector.quantize_mx(out=words.bitcast(FP8X4), scales=scales, in_=grouped[:].rearrange("p c t -> p (c t)"))

        def turn(out, src, opens, closes):
            nc.tensor.matmul(out, src, identity[:], is_transpose=True, start=opens, stop=closes)

        def entries(lst, lo, hi):
            return lst[:, lo // LIST_COLUMN : hi // LIST_COLUMN]

        x_scale_table = tile([P, T], U8, "x_scale_table")
        nc.gpsimd.memset(x_scale_table[:, : T // 2].bitcast(I32), 0)
        nc.vector.memset(x_scale_table[:, T // 2 :].bitcast(I32), 0)
        w1s_raw = zeroed_plane("w1s_raw")
        w2s_raw = zeroed_plane("w2s_raw")
        gain_rows = tile([P, P], F32, "gain_rows")
        nc.vector.memset(gain_rows[:], 0.0)
        identity = tile([P, P], F32, "identity")
        make_identity(nc, identity[:])

        x_word_table = tile([P, T], I32, "x_word_table")
        x_view = x_words[0].rearrange("p c r -> p (c r)").bitcast(I32)
        nc.sync.dma_start(x_word_table[:, :LEAD], x_view[:, :LEAD])
        l_offs = load_list(offs, "l_offs")
        load_scale_rows(x_scale_table, x_scales, (nc.sync, nc.scalar))
        l_two = load_list(two, "l_two")
        nc.sync.dma_start(x_word_table[:, LEAD:], x_view[:, LEAD:])
        w1w_raw = load_weight_words(w1_words, "w1w_raw")
        load_scale_rows(w1s_raw, w1_scales)
        l1 = load_list(n1, "l1")
        l2 = load_list(n2, "l2")
        w2w_raw = load_weight_words(w2_words, "w2w_raw")
        load_scale_rows(w2s_raw, w2_scales)
        for j, gain in enumerate((ga, gb)):
            nc.sync.dma_start(
                gain_rows[PACK * j : PACK * (j + 1), :].rearrange("t (c r) -> t c r", c=BLOCKS),
                gain.rearrange("(c t r) o -> t c (r o)", c=BLOCKS, t=PACK),
            )
        l4 = load_list(n4, "l4")
        l3 = load_list(n3, "l3")
        l5 = load_list(n5, "l5")
        l6 = load_list(n6, "l6")
        l7 = load_list(n7, "l7")

        xb_s = tile([P, V], U8, "xb_s")
        xa_s = tile([P, S], U8, "xa_s")
        xa_w = tile([P, S], U32, "xa_w")
        nc.vector.tensor_copy(xa_s[:], x_scale_table[:].indirect(l_offs[:]))
        nc.vector.tensor_copy(xb_s[:], x_scale_table[:].indirect(l_two[:]))
        nc.vector.tensor_copy(xa_w[:], x_word_table[:].bitcast(U32).indirect(l_offs[:]))
        w1w = deal(w1w_raw, "w1w")
        w1s = deal(w1s_raw, "w1s")
        xb_w = tile([P, V], U32, "xb_w", "w1s_raw")
        nc.vector.tensor_copy(xb_w[:], x_word_table[:].bitcast(U32).indirect(l_two[:]))
        w2w = deal(w2w_raw, "w2w")

        a_ps = [bank([P, S], f"a_ps{t}", t) for t in range(PACK)]
        a_sb = [tile([P, S], F32, f"a_sb{t}") for t in range(PACK)]
        a_ps_high = bank([P, S], "a_ps_high", 7)
        for half_ps, cols in ((a_ps[0], slice(0, HALF)), (a_ps_high, slice(HALF, S))):
            project(half_ps[:, cols], w1w, w1s, 0, xa_w[:, cols], xa_s[:, cols])
            nc.scalar.copy(a_sb[0][:, cols], half_ps[:, cols])
        for t in range(1, PACK):
            project(a_ps[t][:], w1w, w1s, t, xa_w[:], xa_s[:])
            nc.scalar.copy(a_sb[t][:], a_ps[t][:])

        gains_ps = bank([P, P], "gains_ps", 0)
        gains = tile([P, 2 * PACK], F32, "gains")
        nc.tensor.transpose(gains_ps[:], gain_rows[:], identity[:])
        nc.scalar.copy(gains[:], gains_ps[:, : 2 * PACK])
        gb_neg = tile([P, PACK], F32, "gb_neg")
        nc.scalar.activation(gb_neg[:], gains_ps[:, PACK : 2 * PACK], ACT.Copy, scale=-1.0)

        z_grouped = [tile([P, P, PACK], BF16, f"z_grouped{u}") for u in range(PACK)]
        pa, diff, up, down_size, down, dt = {}, {}, {}, {}, {}, {}

        def fetch_first(t, slot_of=None):
            pa[t] = tile([P, W], F32, f"pa{t}", slot_of)
            nc.vector.tensor_copy(pa[t][:], a_sb[t][:].indirect(l1[:]))

        def fetch_difference(t, slot_of=None):
            diff[t] = tile([P, W], F32, f"diff{t}", slot_of)
            nc.vector.tensor_tensor(diff[t][:], a_sb[t][:].indirect(l2[:]), pa[t][:], ALU.subtract)
            down_size[t] = tile([P, W], F32, f"down_size{t}")
            nc.scalar.activation(down_size[t][:], diff[t][:], ACT.Relu, scale=-1.0)

        def step_down(t, slot_of=None):
            down[t] = tile([P, W], F32, f"down{t}", slot_of)
            nc.scalar.activation(down[t][:], down_size[t][:], ACT.Copy, scale=-1.0)

        def step_up(t):
            up[t] = tile([P, W], F32, f"up{t}")
            nc.scalar.activation(up[t][:], diff[t][:], ACT.Relu)

        def put_larger(t, slot_of=None):
            dt[t] = tile([P, S], F32, f"dt{t}", slot_of)
            nc.vector.tensor_tensor(dt[t][:].indirect(l1[:]), pa[t][:], up[t][:], ALU.add)

        def put_smaller(t):
            nc.vector.tensor_tensor(dt[t][:].indirect(l2[:]), pa[t][:], down[t][:], ALU.add)

        def round_z(t):
            for u in range(PACK):
                nc.scalar.activation(z_grouped[u][:, :, t], dt[t][:, u::PACK], ACT.Copy, scale=gains[:, t : t + 1])

        b_ps = [bank([P, V], f"b_ps{t}", PACK + t) for t in range(PACK)]
        b_sb = [tile([P, 2 * V], F32, f"b_sb{t}") for t in range(PACK)]
        b_pos = [tile([P, V], F32, f"b_pos{t}") for t in range(PACK)]
        b_neg = [tile([P, V], F32, f"b_neg{t}") for t in range(PACK)]

        def second_projection(t):
            project(b_ps[t][:], w2w, w2s, t, xb_w[:], xb_s[:])
            nc.scalar.copy(b_sb[t][:, :V], b_ps[t][:])
            nc.scalar.activation(b_pos[t][:], b_ps[t][:], ACT.Copy, scale=gains[:, PACK + t : PACK + t + 1])
            nc.scalar.activation(b_neg[t][:], b_ps[t][:], ACT.Copy, scale=gb_neg[:, t : t + 1])

        def add_terms(t):
            plus = tile([P, V], F32, f"plus{t}")
            minus = tile([P, V], F32, f"minus{t}")
            nc.vector.tensor_tensor(plus[:], b_sb[t][:].indirect(l3[:]), b_pos[t][:], ALU.mult)
            nc.vector.tensor_tensor(minus[:], b_sb[t][:].indirect(l4[:]), b_neg[t][:], ALU.mult)
            for term, opens in ((plus, True), (minus, False)):
                for j in range(PACK):
                    turn(turned[j][:, t, :], term[:, P * j : P * (j + 1)], opens, not opens)

        back = {}

        def round_and_turn_back(j):
            pairs = tile([P, 2, P, 2], BF16, f"pairs{j}")
            nc.scalar.copy(pairs[:], turned[j][:].rearrange("v (w e) p -> v w p e", e=2))
            words = pairs[:].rearrange("v w p e -> v (w p e)").bitcast(F32)
            back[j] = bank([P, 2, P], f"back{j}", j)
            for w in range(2):
                nc.tensor.transpose(back[j][:, w, :], words[:, P * w : P * (w + 1)], identity[:])

        def group_z2(j):
            nc.scalar.copy(
                z2_grouped[:, P * j : P * (j + 1), :].rearrange("p v t -> p (v t)").bitcast(F32).rearrange("p (v w) -> p v w", w=2),
                back[j][:].rearrange("p w v -> p v w"),
            )

        for t in range(2):
            fetch_first(t)
            if t == 1:
                w2s = deal(w2s_raw, "w2s", "a_sb0")
            fetch_difference(t)
            step_down(t)
            step_up(t)
        put_larger(0)
        fetch_first(2, "diff0")
        put_smaller(0)
        round_z(0)
        fetch_difference(2, "up0")
        step_up(2)
        second_projection(0)
        second_projection(1)
        put_larger(1, "w2w")
        fetch_first(3, "diff1")
        put_smaller(1)
        fetch_difference(3, "up1")
        step_up(3)
        second_projection(2)
        second_projection(3)
        round_z(1)

        turned = [bank([P, PACK, P], f"turned{j}", j) for j in range(PACK)]
        for t in range(PACK):
            add_terms(t)
        put_larger(2, "b_pos3")
        put_larger(3, "b_neg3")
        z2_grouped = tile([P, V, PACK], BF16, "z2_grouped")
        for j in range(PACK - 1):
            round_and_turn_back(j)
        step_down(2, "pairs0")
        round_and_turn_back(PACK - 1)
        group_z2(0)
        step_down(3, "pairs2")
        for j in range(1, PACK):
            group_z2(j)
        for t in range(2, PACK):
            put_smaller(t)
            round_z(t)

        z2_w = tile([P, V], U32, "z2_w")
        z2_s = tile([P, V], U8, "z2_s")
        z_w = [tile([P, P], U32, f"z_w{u}") for u in range(PACK)]
        z_s = [tile([P, P], U8, f"z_s{u}") for u in range(PACK)]
        s_ps = [bank([P, V], f"s_ps{u}", PACK + u) for u in range(PACK)]
        s_sb = [tile([P, 2 * V if u < PACK - 1 else V], F32, f"s_sb{u}") for u in range(PACK)]
        sig = [tile([P, V], F32, f"sig{u}") for u in range(PACK)]

        def scores(out, u, cols):
            multiply(out[:, cols], z_w[u][:].bitcast(FP8X4), z_s[u][:], z2_w[:, cols].bitcast(FP8X4), z2_s[:, cols])

        quantize(z2_w[:], z2_s[:], z2_grouped)
        quantize(z_w[0][:], z_s[0][:], z_grouped[0])
        s_ps_high = bank([P, V], "s_ps_high", 0)
        for half_ps, cols in ((s_ps[0], slice(0, HALF)), (s_ps_high, slice(HALF, V))):
            scores(half_ps, 0, cols)
            nc.vector.tensor_scalar(s_sb[0][:, cols], half_ps[:, cols], SCORE_SCALE, None, ALU.mult)
            nc.scalar.activation(sig[0][:, cols], half_ps[:, cols], ACT.Sigmoid, scale=SCORE_SCALE)
        for u in range(1, PACK):
            quantize(z_w[u][:], z_s[u][:], z_grouped[u])
            scores(s_ps[u], u, slice(0, V))

        y_w = tile([P, V], I32, "y_w")
        y_s = tile([P, V], U8, "y_s")
        out_rows = out_0.rearrange("(p u) (g c) -> p u g c", u=PACK, c=P)
        out_words = out_1[0].rearrange("p c r -> p (c r)").bitcast(I32)
        y = tile([P, PACK, PACK, P], F32, "y")
        pieces = [(u, 0, V) for u in range(PACK - 1)] + [(PACK - 1, 0, HALF), (PACK - 1, HALF, V)]
        first, second, sig7 = {}, {}, {}

        def first_term(k):
            u, lo, hi = pieces[k]
            if u > 0:
                if u < VECTOR_COPIES:
                    nc.vector.tensor_scalar(s_sb[u][:, :V], s_ps[u][:], SCORE_SCALE, None, ALU.mult)
                elif lo == 0:
                    nc.scalar.activation(s_sb[u][:, :V], s_ps[u][:], ACT.Copy, scale=SCORE_SCALE)
                nc.scalar.activation(sig[u][:, lo:hi], s_ps[u][:, lo:hi], ACT.Sigmoid, scale=SCORE_SCALE)
            sig7[k] = tile([P, hi - lo], F32, f"sig7_{k}")
            nc.scalar.activation(sig7[k][:], s_sb[u][:].indirect(entries(l7, lo, hi)), ACT.Sigmoid)
            first[k] = tile([P, hi - lo], F32, f"first{k}")
            for c0, c1 in ((0, HALF), (HALF, V)) if u == 0 else ((lo, hi),):
                nc.vector.tensor_tensor(first[k][:, c0 - lo : c1 - lo], s_sb[u][:].indirect(entries(l5, c0, c1)), sig[u][:, c0:c1], ALU.mult)

        def second_term(k):
            u, lo, hi = pieces[k]
            second[k] = tile([P, hi - lo], F32, f"second{k}")
            nc.vector.tensor_tensor(second[k][:], s_sb[u][:].indirect(entries(l6, lo, hi)), sig7[k][:], ALU.mult)

        def add_on_vector(k):
            u, lo, hi = pieces[k]
            groups = slice(lo // P, hi // P)
            nc.vector.tensor_tensor(
                y[:, groups, u, :],
                first[k][:].rearrange("p (g c) -> p g c", c=P),
                second[k][:].rearrange("p (g c) -> p g c", c=P),
                ALU.add,
            )
            nc.sync.dma_start(out_rows[:, u, groups, :], y[:, groups, u, :])

        def add_on_tensor():
            sums = {}
            for u in range(TENSOR_SUMS):
                sum_ps = bank([P, PACK, P], f"sum_ps{u}", 1 + u)
                for g in range(PACK):
                    turn(sum_ps[:, g, :], first[u][:, P * g : P * (g + 1)], True, False)
                    turn(sum_ps[:, g, :], second[u][:, P * g : P * (g + 1)], False, True)
                sums[u] = tile([P, PACK, P], F32, f"sums{u}")
                nc.scalar.copy(sums[u][:], sum_ps[:])
            for u in range(TENSOR_SUMS):
                y_ps = bank([P, PACK, P], f"y_ps{u}", (3 + u) % PACK)
                for g in range(PACK):
                    nc.tensor.transpose(y_ps[:, g, :], sums[u][:, g, :], identity[:])
                nc.scalar.copy(y[:, :, u, :], y_ps[:])
                nc.sync.dma_start(out_rows[:, u, :, :], y[:, :, u, :])

        def regroup(copy, lo, hi):
            grouped = tile([P, hi - lo, PACK], BF16, f"y_grouped{lo}")
            copy(
                grouped[:].rearrange("p (g c i) u -> p g c u i", c=P // 4, i=4),
                y[:, lo // P : hi // P].rearrange("p g u (c i) -> p g c u i", i=4),
            )
            return grouped

        last = len(pieces) - 1
        for k in range(len(pieces)):
            first_term(k)
            if k > TENSOR_SUMS:
                add_on_vector(k - 1)
            if k == last:
                add_on_tensor()
                y_low = regroup(nc.scalar.copy, 0, HALF)
            second_term(k)
        add_on_vector(last)

        third = HALF + P
        y_third = regroup(nc.scalar.copy, HALF, third)
        y_last = regroup(nc.vector.tensor_copy, third, V)
        quantize(y_w[:, :HALF], y_s[:, :HALF], y_low)
        nc.sync.dma_start(out_words[:, :HALF], y_w[:, :HALF])
        quantize(y_w[:, third:], y_s[:, third:], y_last)
        quantize(y_w[:, HALF:third], y_s[:, HALF:third], y_third)
        nc.scalar.dma_start(out_words[:, HALF:], y_w[:, HALF:])
        for q in range(4):
            queue = nc.scalar if q % 2 else nc.sync
            queue.dma_start(out_2[0, 4 * q : 4 * q + 4, :].bitcast(I32), y_s[32 * q : 32 * q + 4, :].bitcast(I32))
